import numpy as np
import ml_dtypes


def mxq(x, axis, fmt="e4m3"):
    dtype, down = {"e4m3": (ml_dtypes.float8_e4m3fn, 7), "e5m2": (ml_dtypes.float8_e5m2, 14)}[fmt]
    v = np.moveaxis(np.asarray(x, np.float32).astype(ml_dtypes.bfloat16).astype(np.float64), axis, -1)
    blocks = v.reshape(v.shape[:-1] + (-1, 32))
    amax = np.abs(blocks).max(-1, keepdims=True)
    byte = np.maximum(np.where(amax > 0, np.frexp(amax)[1] - 1 + 127, 0) - down, 1)
    scale = np.exp2(byte - 127.0)
    codes = (blocks / scale).astype(np.float32).astype(dtype).astype(np.float64)
    return np.moveaxis((codes * scale).reshape(v.shape), -1, axis)


WIDE = False


def mx_kscale(k):
    if not WIDE:
        return np.ones(k)
    levels = np.array([24, -24, 12, -12, 0])
    if k % 512:
        return np.exp2(np.random.permutation(np.resize(levels, k // 32))).repeat(32)
    a = np.empty((k // 512, 16))
    for p in range(k // 512):
        a[p, :8] = np.random.permutation(np.resize(levels, 8))
        for g in range(8):
            far = levels[np.abs(levels - a[p, g]) >= 10]
            a[p, g + 8] = far[np.random.randint(len(far))]
    return np.exp2(a.ravel()).repeat(32)


def f64(x):
    return np.asarray(x).astype(np.float64)


def striped(idx):
    return np.tile(idx.reshape(-1, 16).T, (8, 1)).astype(np.uint16)


def unstriped(offs):
    return offs[:16].T.reshape(-1).astype(np.int64)


E2M1 = np.array([0.0, 0.5, 1.0, 1.5, 2.0, 3.0, 4.0, 6.0, -0.0, -0.5, -1.0, -1.5, -2.0, -3.0, -4.0, -6.0])


def pack_weight(w, fmt):
    k, n = w.shape
    w = f64(np.asarray(w, np.float32).astype(ml_dtypes.bfloat16)).reshape(k // 32, 32, n)
    amax = np.abs(w).max(1)
    if fmt == "e4m3":
        byte = np.frexp(amax)[1] - 1 + 127 - 7
    else:
        mant, ex = np.frexp(amax / 6.0)
        byte = np.where(mant > 0.5, ex, ex - 1) + 127
    byte = np.clip(np.where(amax > 0, byte, 1), 1, 254)
    scaled = (w * np.exp2(127.0 - byte)[:, None, :]).reshape(k, n).astype(np.float32)
    by_word = np.ascontiguousarray(scaled.reshape(k // 512, 128, 4, n).transpose(0, 1, 3, 2))
    if fmt == "e4m3":
        words = by_word.astype(ml_dtypes.float8_e4m3fn).view(np.uint8)
    else:
        c = by_word.astype(ml_dtypes.float4_e2m1fn).view(np.uint8) & 0xF
        words = (c[..., 0::2] | (c[..., 1::2] << 4)).reshape(k // 512, 128, 2 * n)
    return np.ascontiguousarray(words), np.ascontiguousarray(byte.astype(np.uint8).reshape(k // 512, 16, n))


def unpack_weight(words, scales, fmt):
    g, _, n = scales.shape
    words = np.ascontiguousarray(words).reshape(g, 128, n, -1)
    if fmt == "e4m3":
        vals = words.view(ml_dtypes.float8_e4m3fn).astype(np.float64)
    else:
        nib = np.empty((g, 128, n, 4), np.uint8)
        nib[..., 0::2] = words & 0xF
        nib[..., 1::2] = words >> 4
        vals = E2M1[nib]
    vals = vals * np.repeat(np.exp2(scales.astype(np.float64) - 127.0), 8, axis=1)[..., None]
    return vals.transpose(0, 1, 3, 2).reshape(g * 512, n)


K, R, M, T, N, J = 512, 1024, 256, 2048, 512, 1024


def setup_inputs():
    n = np.random.standard_normal
    u = mx_kscale(R)[:, None]
    s = mx_kscale(K)[:, None]
    w = n((K, R)) / np.sqrt(K) / s / u.T
    w4 = pack_weight(w, "e2m1")
    rest = w - unpack_weight(*w4, "e2m1")
    wv = n((R, N)) / np.sqrt(R) / u
    p_r8 = pack_weight(rest, "e4m3")
    p_tab = pack_weight(n((R, T)) * u, "e4m3")
    p_wv4 = pack_weight(wv[512:], "e2m1")
    return {
        "x": (n((K, M)) * s).astype(np.float32),
        "w4_words": w4[0],
        "w4_scales": w4[1],
        "r8_words": p_r8[0],
        "r8_scales": p_r8[1],
        "tab_words": p_tab[0],
        "tab_scales": p_tab[1],
        "wv8": (wv[:512]).astype(np.float32),
        "wv4_words": p_wv4[0],
        "wv4_scales": p_wv4[1],
        "msk": (np.where(np.random.rand(M, J) < 0.2, -4.0, 0.0)).astype(np.float32),
        "offs": striped(np.random.permutation(T)[:J]),
    }


def reference(x, w4_words, w4_scales, r8_words, r8_scales, tab_words, tab_scales, wv8, wv4_words, wv4_scales, msk, offs):
    idx = unstriped(offs)
    x_ = mxq(f64(x), 0, "e4m3")
    w4_ = unpack_weight(w4_words, w4_scales, "e2m1")
    r8_ = unpack_weight(r8_words, r8_scales, "e4m3")
    qa = w4_.T @ x_ + r8_.T @ x_
    qa_ = mxq(qa, 0, "e4m3")
    tab_ = unpack_weight(tab_words, tab_scales, "e4m3")[:, idx]
    sc = qa_.T @ tab_
    wv8_ = mxq(f64(wv8), 0, "e4m3")
    wv4_ = unpack_weight(wv4_words, wv4_scales, "e2m1")
    vv = wv8_.T @ tab_[:512] + wv4_.T @ tab_[512:]
    return sc * 0.03125 + f64(msk), vv

@@ -1,0 +1,225 @@
+from contextlib import ExitStack
+
+import concourse.mybir as mybir
+from concourse.masks import make_identity
+
+K, R, M, T, N, J = 512, 1024, 256, 2048, 512, 1024
+FLOPS = 2 * (2 * K * R * M + R * M * J + R * N * J)
+SCORE_SCALE = 0.03125
+
+F32 = mybir.dt.float32
+BF16 = mybir.dt.bfloat16
+I32 = mybir.dt.int32
+U32 = mybir.dt.uint32
+U16 = mybir.dt.uint16
+U8 = mybir.dt.uint8
+E4M3 = mybir.dt.float8_e4m3fn_x4
+E2M1 = mybir.dt.float4_e2m1fn_x4
+MULT = mybir.AluOpType.mult
+ADD = mybir.AluOpType.add
+
+P = 128
+PACK = 4
+BANK = 512
+HALF = J // 2
+SECOND = 4
+
+
+def load_scale_rows(queue, plane, first_row, rows):
+    for q in range(4):
+        lo = 32 * q + first_row
+        queue.dma_start(out=plane[lo : lo + 4, :].bitcast(I32), in_=rows[4 * q : 4 * q + 4, :].bitcast(I32))
+
+
+def interleave(copy, grouped, raw):
+    copy(
+        out=grouped.rearrange("p (c i) j -> p c j i", i=4),
+        in_=raw.rearrange("p j (c i) -> p c j i", i=4),
+    )
+
+
+def tile_list_mlat_resid_qf_mask_kernel(
+    tc, x, w4_words, w4_scales, r8_words, r8_scales, tab_words, tab_scales, wv8, wv4_words, wv4_scales, msk, offs, out_0, out_1
+):
+    nc = tc.nc
+    with ExitStack() as ctx:
+        sb = ctx.enter_context(tc.tile_pool(name="sb", bufs=1))
+        ps = ctx.enter_context(tc.psum_pool(name="ps", bufs=1))
+
+        def tile(name, shape, dtype, tag=None):
+            return sb.tile(shape, dtype, name=name, tag=tag or name, align_bytes=64)
+
+        def bank(index, shape):
+            return ps.tile(shape, F32, name="bank%d" % index, tag="bank%d" % index)
+
+        offsets = sb.tile([P, J // 16], U16, name="offsets")
+        w_plane = tile("w_plane", [P, R], U8)
+        tab_plane = tile("tab_plane", [P, T], U8)
+        wv4_plane = tile("wv4_plane", [P, N], U8)
+        nc.vector.memset(tab_plane[:].bitcast(I32), 0)
+
+        x_raw = tile("x_raw", [P, PACK, M], F32)
+        r8 = tile("r8", [P, R], U32)
+        w4 = tile("w4", [P, 2 * R], U8)
+        tab = [tile("tab%d" % a, [P, T], U32) for a in range(2)]
+        wv4 = tile("wv4", [P, 2 * N], U8)
+        wv8_raw = tile("wv8_raw", [P, PACK, N], F32)
+        mask = [tile("mask%d" % t, [P, J], F32) for t in range(2)]
+
+        def load_table_half(a, half):
+            cols = slice(half * T // 2, (half + 1) * T // 2)
+            nc.sync.dma_start(out=tab[a][:, cols].bitcast(I32), in_=tab_words[a].rearrange("p t i -> p (t i)").bitcast(I32)[:, cols])
+
+        load_scale_rows(nc.gpsimd, w_plane, SECOND, r8_scales[0])
+        nc.sync.dma_start(out=x_raw[:], in_=x.rearrange("(p j) m -> p j m", j=PACK))
+        load_scale_rows(nc.sync, tab_plane, 0, tab_scales[1])
+        nc.sync.dma_start(offsets[:], offs)
+        nc.sync.dma_start(out=w4[:].bitcast(I32), in_=w4_words[0].bitcast(I32))
+        nc.sync.dma_start(out=r8[:].bitcast(I32), in_=r8_words[0].rearrange("p r i -> p (r i)").bitcast(I32))
+        load_scale_rows(nc.sync, tab_plane, SECOND, tab_scales[0])
+        load_table_half(1, 0)
+        load_scale_rows(nc.sync, w_plane, 0, w4_scales[0])
+        load_table_half(1, 1)
+        load_table_half(0, 0)
+        nc.sync.dma_start(out=wv4[:].bitcast(I32), in_=wv4_words[0].bitcast(I32))
+        load_scale_rows(nc.sync, wv4_plane, 0, wv4_scales[0])
+        load_table_half(0, 1)
+        nc.sync.dma_start(out=mask[0][:], in_=msk[0:P, :])
+        nc.sync.dma_start(out=wv8_raw[:], in_=wv8.rearrange("(p j) n -> p j n", j=PACK))
+        nc.sync.dma_start(out=mask[1][:], in_=msk[P : 2 * P, :])
+        ident = tile("ident", [P, P], F32)
+        make_identity(nc, ident[:])
+
+        x_grouped = [tile("x_grouped%d" % t, [P, P, PACK], BF16) for t in range(2)]
+        x_codes = [tile("x_codes%d" % t, [P, P], U32) for t in range(2)]
+        x_plane = [tile("x_plane%d" % t, [P, P], U8) for t in range(2)]
+        for t in range(2):
+            interleave(nc.vector.tensor_copy, x_grouped[t][:], x_raw[:, :, t * P : (t + 1) * P])
+        for t in range(2):
+            nc.vector.quantize_mx(
+                out=x_codes[t][:].bitcast(E4M3), scales=x_plane[t][:], in_=x_grouped[t][:].rearrange("p m j -> p (m j)")
+            )
+
+        qa_rows = []
+        for t in range(2):
+            for a in range(2):
+                acc = bank(2 * t + a, [P, BANK])
+                nc.tensor.matmul_mx(
+                    out=acc[:], lhsT=x_codes[t][:].bitcast(E4M3), lhsT_scale=x_plane[t][:],
+                    rhs=w4[:, 2 * BANK * a : 2 * BANK * (a + 1)].bitcast(E2M1), rhs_scale=w_plane[:, BANK * a : BANK * (a + 1)],
+                    start=True, stop=False,
+                )
+                nc.tensor.matmul_mx(
+                    out=acc[:], lhsT=x_codes[t][:].bitcast(E4M3), lhsT_scale=x_plane[t][:],
+                    rhs=r8[:, BANK * a : BANK * (a + 1)].bitcast(E4M3), rhs_scale=w_plane[SECOND:, BANK * a : BANK * (a + 1)],
+                    start=False, stop=True,
+                )
+                rows = tile("qa_rows%d%d" % (t, a), [P, 2, P, 2], BF16)
+                nc.scalar.copy(out=rows[:], in_=acc[:].rearrange("m (p u e) -> m u p e", u=2, e=2))
+                qa_rows.append(rows)
+
+        qa_grouped = []
+        for t in range(2):
+            turned = bank(4 + t, [P, 2, 2, P])
+            for a in range(2):
+                words = qa_rows[2 * t + a][:].rearrange("m u p e -> m (u p e)").bitcast(F32)
+                for u in range(2):
+                    nc.tensor.transpose(turned[:, a, u, :], words[:, u * P : (u + 1) * P], ident[:])
+            grouped = tile("qa_grouped%d" % t, [P, 2 * P * PACK], BF16)
+            nc.scalar.copy(
+                out=grouped[:].bitcast(F32).rearrange("p (a m u) -> p a m u", a=2, u=2),
+                in_=turned[:].rearrange("p a u m -> p a m u"),
+            )
+            qa_grouped.append(grouped)
+
+        got_plane = [tile("got_plane%d" % h, [P, HALF], U8, "x_grouped%d" % h) for h in range(2)]
+        got = [[tile("got%d%d" % (a, h), [P, HALF], U32) for h in range(2)] for a in range(2)]
+        lists = [offsets[:, h * (HALF // 16) : (h + 1) * (HALF // 16)] for h in range(2)]
+        for h in range(2):
+            nc.vector.tensor_copy(got_plane[h][:], tab_plane[:].indirect(lists[h]))
+        for h in range(2):
+            nc.vector.tensor_copy(got[1][h][:], tab[1][:].indirect(lists[h]))
+
+        for h in range(2):
+            nc.vector.tensor_copy(got[0][h][:], tab[0][:].indirect(lists[h]))
+        qa_both = tile("qa_both", [P, 4 * P], U32, "tab0")
+        qa_codes = [qa_both[:, 2 * P * t : 2 * P * (t + 1)] for t in range(2)]
+        qa_plane = [tile("qa_plane%d" % t, [P, 2 * P], U8) for t in range(2)]
+        for t in range(2):
+            nc.vector.quantize_mx(out=qa_codes[t].bitcast(E4M3), scales=qa_plane[t][:], in_=qa_grouped[t][:])
+
+
+        def wv4_pass(acc, n, h):
+            nc.tensor.matmul_mx(
+                out=acc[:], lhsT=wv4[:, 2 * P * n : 2 * P * (n + 1)].bitcast(E2M1), lhsT_scale=wv4_plane[:, P * n : P * (n + 1)],
+                rhs=got[1][h][:].bitcast(E4M3), rhs_scale=got_plane[h][:], start=True, stop=False,
+            )
+
+        def score_pass(acc, t, a, h):
+            first_row = SECOND * (1 - a)
+            nc.tensor.matmul_mx(
+                out=acc[:], lhsT=qa_codes[t][:, P * a : P * (a + 1)].bitcast(E4M3), lhsT_scale=qa_plane[t][:, P * a : P * (a + 1)],
+                rhs=got[a][h][:].bitcast(E4M3), rhs_scale=got_plane[h][first_row:, :], start=(a == 1), stop=(a == 0),
+            )
+
+        value_bank = {(0, 0): 0, (1, 0): 1, (0, 1): 2, (1, 1): 3, (2, 0): 6, (2, 1): 7, (3, 0): 0, (3, 1): 2}
+        value_acc = {}
+        for h in range(2):
+            for n in range(2):
+                value_acc[n, h] = bank(value_bank[n, h], [P, BANK])
+                wv4_pass(value_acc[n, h], n, h)
+
+        score_acc = {}
+        for t in range(2):
+            for h in range(2):
+                score_acc[t, h] = bank(6 - 2 * t + h, [P, BANK])
+                score_pass(score_acc[t, h], t, 1, h)
+                score_pass(score_acc[t, h], t, 0, h)
+
+        wv8_grouped = [tile("wv8_grouped%d" % n, [P, P, PACK], BF16) for n in range(4)]
+        wv8_codes = [tile("wv8_codes%d" % n, [P, P], U32) for n in range(4)]
+        wv8_plane = [tile("wv8_plane%d" % n, [P, P], U8) for n in range(4)]
+        for n in range(4):
+            copy = nc.scalar.copy if n < 2 else nc.vector.tensor_copy
+            interleave(copy, wv8_grouped[n][:], wv8_raw[:, :, n * P : (n + 1) * P])
+        for n in range(4):
+            nc.vector.quantize_mx(
+                out=wv8_codes[n][:].bitcast(E4M3), scales=wv8_plane[n][:], in_=wv8_grouped[n][:].rearrange("p n j -> p (n j)")
+            )
+
+        def wv8_pass(acc, n, h):
+            nc.tensor.matmul_mx(
+                out=acc[:], lhsT=wv8_codes[n][:].bitcast(E4M3), lhsT_scale=wv8_plane[n][:],
+                rhs=got[0][h][:].bitcast(E4M3), rhs_scale=got_plane[h][SECOND:, :], start=False, stop=True,
+            )
+
+        def store_values(n):
+            result = tile("values%d" % n, [P, J], F32)
+            for h in range(2):
+                wv8_pass(value_acc[n, h], n, h)
+            for h in range(2):
+                copy = nc.vector.tensor_copy if (n >= 2 and h == 1) else nc.scalar.copy
+                copy(out=result[:, h * HALF : (h + 1) * HALF], in_=value_acc[n, h][:])
+            nc.sync.dma_start(out=out_1[n * P : (n + 1) * P, :], in_=result[:])
+
+        def store_scores(t):
+            result = tile("scores%d" % t, [P, J], F32)
+            for h in range(2):
+                cols = slice(h * HALF, (h + 1) * HALF)
+                nc.vector.scalar_tensor_tensor(
+                    out=result[:, cols], in0=score_acc[t, h][:], scalar=SCORE_SCALE, in1=mask[t][:, cols], op0=MULT, op1=ADD
+                )
+                if t == 0:
+                    nc.sync.dma_start(out=out_0[0:P, cols], in_=result[:, cols])
+            if t == 1:
+                nc.sync.dma_start(out=out_0[P : 2 * P, :], in_=result[:])
+
+        store_scores(0)
+        store_values(0)
+        store_scores(1)
+        store_values(1)
+        for n in range(2, 4):
+            for h in range(2):
+                value_acc[n, h] = bank(value_bank[n, h], [P, BANK])
+                wv4_pass(value_acc[n, h], n, h)
+            store_values(n)

@@ -22,13 +22,14 @@ P = 128
 PACK = 4
 BANK = 512
 HALF = J // 2
-SECOND = 4
+TAB_ROW = (4, 0)
+R8_ROW = 8
 
 
 def load_scale_rows(queue, plane, first_row, rows):
-    for q in range(4):
-        lo = 32 * q + first_row
-        queue.dma_start(out=plane[lo : lo + 4, :].bitcast(I32), in_=rows[4 * q : 4 * q + 4, :].bitcast(I32))
+    by_place = rows.rearrange("(q r) n -> r q n", r=4)
+    for r in range(4):
+        queue.dma_start(out=plane[first_row + r : P : 32, :].bitcast(I32), in_=by_place[r].bitcast(I32))
 
 
 def interleave(copy, grouped, raw):
@@ -46,49 +47,49 @@ def tile_list_mlat_resid_qf_mask_kernel(
         sb = ctx.enter_context(tc.tile_pool(name="sb", bufs=1))
         ps = ctx.enter_context(tc.psum_pool(name="ps", bufs=1))
 
-        def tile(name, shape, dtype, tag=None):
-            return sb.tile(shape, dtype, name=name, tag=tag or name, align_bytes=64)
+        def tile(name, shape, dtype, reuses=None):
+            return sb.tile(shape, dtype, name=name, tag=reuses or name, align_bytes=64)
 
         def bank(index, shape):
             return ps.tile(shape, F32, name="bank%d" % index, tag="bank%d" % index)
 
         offsets = sb.tile([P, J // 16], U16, name="offsets")
-        w_plane = tile("w_plane", [P, R], U8)
+        w4_plane = tile("w4_plane", [P, R], U8)
+        r8_plane = tile("r8_plane", [P, R], U8)
         tab_plane = tile("tab_plane", [P, T], U8)
         wv4_plane = tile("wv4_plane", [P, N], U8)
-        nc.vector.memset(tab_plane[:].bitcast(I32), 0)
-
         x_raw = tile("x_raw", [P, PACK, M], F32)
         r8 = tile("r8", [P, R], U32)
         w4 = tile("w4", [P, 2 * R], U8)
         tab = [tile("tab%d" % a, [P, T], U32) for a in range(2)]
         wv4 = tile("wv4", [P, 2 * N], U8)
-        wv8_raw = tile("wv8_raw", [P, PACK, N], F32)
+        wv8_raw = [tile("wv8_raw%d" % g, [P, PACK, N // 2], F32) for g in range(2)]
         mask = [tile("mask%d" % t, [P, J], F32) for t in range(2)]
-
-        def load_table_half(a, half):
-            cols = slice(half * T // 2, (half + 1) * T // 2)
-            nc.sync.dma_start(out=tab[a][:, cols].bitcast(I32), in_=tab_words[a].rearrange("p t i -> p (t i)").bitcast(I32)[:, cols])
-
-        load_scale_rows(nc.gpsimd, w_plane, SECOND, r8_scales[0])
-        nc.sync.dma_start(out=x_raw[:], in_=x.rearrange("(p j) m -> p j m", j=PACK))
-        load_scale_rows(nc.sync, tab_plane, 0, tab_scales[1])
-        nc.sync.dma_start(offsets[:], offs)
-        nc.sync.dma_start(out=w4[:].bitcast(I32), in_=w4_words[0].bitcast(I32))
-        nc.sync.dma_start(out=r8[:].bitcast(I32), in_=r8_words[0].rearrange("p r i -> p (r i)").bitcast(I32))
-        load_scale_rows(nc.sync, tab_plane, SECOND, tab_scales[0])
-        load_table_half(1, 0)
-        load_scale_rows(nc.sync, w_plane, 0, w4_scales[0])
-        load_table_half(1, 1)
-        load_table_half(0, 0)
-        nc.sync.dma_start(out=wv4[:].bitcast(I32), in_=wv4_words[0].bitcast(I32))
-        load_scale_rows(nc.sync, wv4_plane, 0, wv4_scales[0])
-        load_table_half(0, 1)
-        nc.sync.dma_start(out=mask[0][:], in_=msk[0:P, :])
-        nc.sync.dma_start(out=wv8_raw[:], in_=wv8.rearrange("(p j) n -> p j n", j=PACK))
-        nc.sync.dma_start(out=mask[1][:], in_=msk[P : 2 * P, :])
         ident = tile("ident", [P, P], F32)
+
+        tab_rows = [tab_words[a].rearrange("p t i -> p (t i)").bitcast(I32) for a in range(2)]
+        wv8_rows = wv8.rearrange("(p j) n -> p j n", j=PACK)
+
+        nc.gpsimd.memset(tab_plane[:].bitcast(I32), 0)
+        load_scale_rows(nc.gpsimd, tab_plane, TAB_ROW[0], tab_scales[0])
         make_identity(nc, ident[:])
+
+        nc.sync.dma_start(offsets[:], offs)
+        load_scale_rows(nc.sync, w4_plane, 0, w4_scales[0])
+        nc.sync.dma_start(out=x_raw[:], in_=x.rearrange("(p j) m -> p j m", j=PACK))
+        nc.sync.dma_start(out=w4[:].bitcast(I32), in_=w4_words[0].bitcast(I32))
+        nc.sync.dma_start(out=tab[1][:].bitcast(I32), in_=tab_rows[1])
+        load_scale_rows(nc.sync, r8_plane, R8_ROW, r8_scales[0])
+        nc.sync.dma_start(out=r8[:].bitcast(I32), in_=r8_words[0].rearrange("p r i -> p (r i)").bitcast(I32))
+        nc.sync.dma_start(out=tab[0][:, 0 : T // 2].bitcast(I32), in_=tab_rows[0][:, 0 : T // 2])
+        load_scale_rows(nc.sync, tab_plane, TAB_ROW[1], tab_scales[1])
+        nc.sync.dma_start(out=tab[0][:, T // 2 : T].bitcast(I32), in_=tab_rows[0][:, T // 2 : T])
+        nc.sync.dma_start(out=wv4[:].bitcast(I32), in_=wv4_words[0].bitcast(I32))
+        nc.sync.dma_start(out=wv8_raw[0][:], in_=wv8_rows[:, :, 0 : N // 2])
+        load_scale_rows(nc.sync, wv4_plane, 0, wv4_scales[0])
+        nc.sync.dma_start(out=wv8_raw[1][:], in_=wv8_rows[:, :, N // 2 : N])
+        for t in range(2):
+            nc.sync.dma_start(out=mask[t][:], in_=msk[t * P : (t + 1) * P, :])
 
         x_grouped = [tile("x_grouped%d" % t, [P, P, PACK], BF16) for t in range(2)]
         x_codes = [tile("x_codes%d" % t, [P, P], U32) for t in range(2)]
@@ -100,31 +101,33 @@ def tile_list_mlat_resid_qf_mask_kernel(
                 out=x_codes[t][:].bitcast(E4M3), scales=x_plane[t][:], in_=x_grouped[t][:].rearrange("p m j -> p (m j)")
             )
 
-        qa_rows = []
+        qa_acc = {}
         for t in range(2):
             for a in range(2):
-                acc = bank(2 * t + a, [P, BANK])
+                qa_acc[t, a] = bank(2 * t + a, [P, BANK])
                 nc.tensor.matmul_mx(
-                    out=acc[:], lhsT=x_codes[t][:].bitcast(E4M3), lhsT_scale=x_plane[t][:],
-                    rhs=w4[:, 2 * BANK * a : 2 * BANK * (a + 1)].bitcast(E2M1), rhs_scale=w_plane[:, BANK * a : BANK * (a + 1)],
+                    out=qa_acc[t, a][:], lhsT=x_codes[t][:].bitcast(E4M3), lhsT_scale=x_plane[t][:],
+                    rhs=w4[:, 2 * BANK * a : 2 * BANK * (a + 1)].bitcast(E2M1), rhs_scale=w4_plane[:, BANK * a : BANK * (a + 1)],
                     start=True, stop=False,
                 )
+        qa_rows = {}
+        for t in range(2):
+            for a in range(2):
                 nc.tensor.matmul_mx(
-                    out=acc[:], lhsT=x_codes[t][:].bitcast(E4M3), lhsT_scale=x_plane[t][:],
-                    rhs=r8[:, BANK * a : BANK * (a + 1)].bitcast(E4M3), rhs_scale=w_plane[SECOND:, BANK * a : BANK * (a + 1)],
+                    out=qa_acc[t, a][:], lhsT=x_codes[t][:].bitcast(E4M3), lhsT_scale=x_plane[t][:],
+                    rhs=r8[:, BANK * a : BANK * (a + 1)].bitcast(E4M3), rhs_scale=r8_plane[R8_ROW:, BANK * a : BANK * (a + 1)],
                     start=False, stop=True,
                 )
-                rows = tile("qa_rows%d%d" % (t, a), [P, 2, P, 2], BF16)
-                nc.scalar.copy(out=rows[:], in_=acc[:].rearrange("m (p u e) -> m u p e", u=2, e=2))
-                qa_rows.append(rows)
+                qa_rows[t, a] = tile("qa_rows%d%d" % (t, a), [P, 2, P, 2], BF16)
+                nc.scalar.copy(out=qa_rows[t, a][:], in_=qa_acc[t, a][:].rearrange("m (p u e) -> m u p e", u=2, e=2))
 
         qa_grouped = []
         for t in range(2):
             turned = bank(4 + t, [P, 2, 2, P])
             for a in range(2):
-                words = qa_rows[2 * t + a][:].rearrange("m u p e -> m (u p e)").bitcast(F32)
+                pairs = qa_rows[t, a][:].rearrange("m u p e -> m (u p e)").bitcast(F32)
                 for u in range(2):
-                    nc.tensor.transpose(turned[:, a, u, :], words[:, u * P : (u + 1) * P], ident[:])
+                    nc.tensor.transpose(turned[:, a, u, :], pairs[:, u * P : (u + 1) * P], ident[:])
             grouped = tile("qa_grouped%d" % t, [P, 2 * P * PACK], BF16)
             nc.scalar.copy(
                 out=grouped[:].bitcast(F32).rearrange("p (a m u) -> p a m u", a=2, u=2),
@@ -132,94 +135,103 @@ def tile_list_mlat_resid_qf_mask_kernel(
             )
             qa_grouped.append(grouped)
 
-        got_plane = [tile("got_plane%d" % h, [P, HALF], U8, "x_grouped%d" % h) for h in range(2)]
-        got = [[tile("got%d%d" % (a, h), [P, HALF], U32) for h in range(2)] for a in range(2)]
         lists = [offsets[:, h * (HALF // 16) : (h + 1) * (HALF // 16)] for h in range(2)]
-        for h in range(2):
-            nc.vector.tensor_copy(got_plane[h][:], tab_plane[:].indirect(lists[h]))
-        for h in range(2):
-            nc.vector.tensor_copy(got[1][h][:], tab[1][:].indirect(lists[h]))
+        got = {}
+        got_plane = {}
 
-        for h in range(2):
-            nc.vector.tensor_copy(got[0][h][:], tab[0][:].indirect(lists[h]))
+        def gather_words(a, h, reuses):
+            got[a, h] = tile("got%d%d" % (a, h), [P, HALF], U32, reuses)
+            nc.vector.tensor_copy(got[a, h][:], tab[a][:].indirect(lists[h]))
+
+        def gather_scales(h, reuses):
+            got_plane[h] = tile("got_plane%d" % h, [P, HALF], U8, reuses)
+            nc.vector.tensor_copy(got_plane[h][:], tab_plane[:].indirect(lists[h]))
+
+        gather_words(1, 0, None)
+        gather_words(1, 1, None)
+        gather_scales(0, "tab1")
+        gather_scales(1, None)
+        gather_words(0, 0, None)
+
+        wv8_grouped = [tile("wv8_grouped%d" % n, [P, P, PACK], BF16) for n in range(4)]
+        wv8_codes = [tile("wv8_codes%d" % n, [P, P], U32) for n in range(4)]
+        wv8_plane = [tile("wv8_plane%d" % n, [P, P], U8) for n in range(4)]
+
+        def cast_wv8(n):
+            interleave(nc.scalar.copy, wv8_grouped[n][:], wv8_raw[n // 2][:, :, (n % 2) * P : (n % 2 + 1) * P])
+
+        def quantize_wv8(n):
+            nc.vector.quantize_mx(
+                out=wv8_codes[n][:].bitcast(E4M3), scales=wv8_plane[n][:], in_=wv8_grouped[n][:].rearrange("p n j -> p (n j)")
+            )
+
+        for n in range(2):
+            cast_wv8(n)
+            quantize_wv8(n)
+        gather_words(0, 1, "wv8_grouped1")
+
         qa_both = tile("qa_both", [P, 4 * P], U32, "tab0")
         qa_codes = [qa_both[:, 2 * P * t : 2 * P * (t + 1)] for t in range(2)]
         qa_plane = [tile("qa_plane%d" % t, [P, 2 * P], U8) for t in range(2)]
         for t in range(2):
             nc.vector.quantize_mx(out=qa_codes[t].bitcast(E4M3), scales=qa_plane[t][:], in_=qa_grouped[t][:])
 
-
-        def wv4_pass(acc, n, h):
-            nc.tensor.matmul_mx(
-                out=acc[:], lhsT=wv4[:, 2 * P * n : 2 * P * (n + 1)].bitcast(E2M1), lhsT_scale=wv4_plane[:, P * n : P * (n + 1)],
-                rhs=got[1][h][:].bitcast(E4M3), rhs_scale=got_plane[h][:], start=True, stop=False,
-            )
-
-        def score_pass(acc, t, a, h):
-            first_row = SECOND * (1 - a)
-            nc.tensor.matmul_mx(
-                out=acc[:], lhsT=qa_codes[t][:, P * a : P * (a + 1)].bitcast(E4M3), lhsT_scale=qa_plane[t][:, P * a : P * (a + 1)],
-                rhs=got[a][h][:].bitcast(E4M3), rhs_scale=got_plane[h][first_row:, :], start=(a == 1), stop=(a == 0),
-            )
-
-        value_bank = {(0, 0): 0, (1, 0): 1, (0, 1): 2, (1, 1): 3, (2, 0): 6, (2, 1): 7, (3, 0): 0, (3, 1): 2}
         value_acc = {}
+        score_acc = {}
+
+        def wv4_pass(n, h):
+            value_acc[n, h] = bank(2 * h + n % 2, [P, BANK])
+            nc.tensor.matmul_mx(
+                out=value_acc[n, h][:], lhsT=wv4[:, 2 * P * n : 2 * P * (n + 1)].bitcast(E2M1),
+                lhsT_scale=wv4_plane[:, P * n : P * (n + 1)],
+                rhs=got[1, h][:].bitcast(E4M3), rhs_scale=got_plane[h][TAB_ROW[1] :, :], start=True, stop=False,
+            )
+
+        def wv8_pass(n, h):
+            nc.tensor.matmul_mx(
+                out=value_acc[n, h][:], lhsT=wv8_codes[n][:].bitcast(E4M3), lhsT_scale=wv8_plane[n][:],
+                rhs=got[0, h][:].bitcast(E4M3), rhs_scale=got_plane[h][TAB_ROW[0] :, :], start=False, stop=True,
+            )
+
+        def store_values(n, h, copy):
+            result = tile("values%d%d" % (n, h), [P, HALF], F32)
+            copy(out=result[:], in_=value_acc[n, h][:])
+            nc.sync.dma_start(out=out_1[n * P : (n + 1) * P, h * HALF : (h + 1) * HALF], in_=result[:])
+
+        def score_passes(t, h):
+            score_acc[t, h] = bank(6 - 2 * t + h, [P, BANK])
+            for a in (1, 0):
+                nc.tensor.matmul_mx(
+                    out=score_acc[t, h][:], lhsT=qa_codes[t][:, P * a : P * (a + 1)].bitcast(E4M3),
+                    lhsT_scale=qa_plane[t][:, P * a : P * (a + 1)],
+                    rhs=got[a, h][:].bitcast(E4M3), rhs_scale=got_plane[h][TAB_ROW[a] :, :], start=(a == 1), stop=(a == 0),
+                )
+
+        def store_scores(t, h):
+            cols = slice(h * HALF, (h + 1) * HALF)
+            result = tile("scores%d%d" % (t, h), [P, HALF], F32)
+            nc.vector.scalar_tensor_tensor(
+                out=result[:], in0=score_acc[t, h][:], scalar=SCORE_SCALE, in1=mask[t][:, cols], op0=MULT, op1=ADD
+            )
+            nc.sync.dma_start(out=out_0[t * P : (t + 1) * P, cols], in_=result[:])
+
         for h in range(2):
             for n in range(2):
-                value_acc[n, h] = bank(value_bank[n, h], [P, BANK])
-                wv4_pass(value_acc[n, h], n, h)
-
-        score_acc = {}
-        for t in range(2):
-            for h in range(2):
-                score_acc[t, h] = bank(6 - 2 * t + h, [P, BANK])
-                score_pass(score_acc[t, h], t, 1, h)
-                score_pass(score_acc[t, h], t, 0, h)
-
-        wv8_grouped = [tile("wv8_grouped%d" % n, [P, P, PACK], BF16) for n in range(4)]
-        wv8_codes = [tile("wv8_codes%d" % n, [P, P], U32) for n in range(4)]
-        wv8_plane = [tile("wv8_plane%d" % n, [P, P], U8) for n in range(4)]
-        for n in range(4):
-            copy = nc.scalar.copy if n < 2 else nc.vector.tensor_copy
-            interleave(copy, wv8_grouped[n][:], wv8_raw[:, :, n * P : (n + 1) * P])
-        for n in range(4):
-            nc.vector.quantize_mx(
-                out=wv8_codes[n][:].bitcast(E4M3), scales=wv8_plane[n][:], in_=wv8_grouped[n][:].rearrange("p n j -> p (n j)")
-            )
-
-        def wv8_pass(acc, n, h):
-            nc.tensor.matmul_mx(
-                out=acc[:], lhsT=wv8_codes[n][:].bitcast(E4M3), lhsT_scale=wv8_plane[n][:],
-                rhs=got[0][h][:].bitcast(E4M3), rhs_scale=got_plane[h][SECOND:, :], start=False, stop=True,
-            )
-
-        def store_values(n):
-            result = tile("values%d" % n, [P, J], F32)
-            for h in range(2):
-                wv8_pass(value_acc[n, h], n, h)
-            for h in range(2):
-                copy = nc.vector.tensor_copy if (n >= 2 and h == 1) else nc.scalar.copy
-                copy(out=result[:, h * HALF : (h + 1) * HALF], in_=value_acc[n, h][:])
-            nc.sync.dma_start(out=out_1[n * P : (n + 1) * P, :], in_=result[:])
-
-        def store_scores(t):
-            result = tile("scores%d" % t, [P, J], F32)
-            for h in range(2):
-                cols = slice(h * HALF, (h + 1) * HALF)
-                nc.vector.scalar_tensor_tensor(
-                    out=result[:, cols], in0=score_acc[t, h][:], scalar=SCORE_SCALE, in1=mask[t][:, cols], op0=MULT, op1=ADD
-                )
-                if t == 0:
-                    nc.sync.dma_start(out=out_0[0:P, cols], in_=result[:, cols])
-            if t == 1:
-                nc.sync.dma_start(out=out_0[P : 2 * P, :], in_=result[:])
-
-        store_scores(0)
-        store_values(0)
-        store_scores(1)
-        store_values(1)
+                wv4_pass(n, h)
+        for h in range(2):
+            for n in range(2):
+                wv8_pass(n, h)
+                store_values(n, h, nc.scalar.copy)
+            cast_wv8(2 + h)
+        for h in range(2):
+            score_passes(0, h)
+            store_scores(0, h)
+            quantize_wv8(2 + h)
+        for h in range(2):
+            score_passes(1, h)
+            store_scores(1, h)
         for n in range(2, 4):
             for h in range(2):
-                value_acc[n, h] = bank(value_bank[n, h], [P, BANK])
-                wv4_pass(value_acc[n, h], n, h)
-            store_values(n)
+                wv4_pass(n, h)
+                wv8_pass(n, h)
+                store_values(n, h, nc.vector.tensor_copy if (n, h) == (3, 1) else nc.scalar.copy)

@@ -74,9 +74,9 @@ def tile_list_mlat_resid_qf_mask_kernel(
         load_scale_rows(nc.gpsimd, tab_plane, TAB_ROW[0], tab_scales[0])
         make_identity(nc, ident[:])
 
-        nc.sync.dma_start(offsets[:], offs)
-        load_scale_rows(nc.sync, w4_plane, 0, w4_scales[0])
         nc.sync.dma_start(out=x_raw[:], in_=x.rearrange("(p j) m -> p j m", j=PACK))
+        load_scale_rows(nc.sync, w4_plane, 0, w4_scales[0])
+        nc.sync.dma_start(offsets[:], offs)
         nc.sync.dma_start(out=w4[:].bitcast(I32), in_=w4_words[0].bitcast(I32))
         nc.sync.dma_start(out=tab[1][:].bitcast(I32), in_=tab_rows[1])
         load_scale_rows(nc.sync, r8_plane, R8_ROW, r8_scales[0])
@@ -135,6 +135,13 @@ def tile_list_mlat_resid_qf_mask_kernel(
             )
             qa_grouped.append(grouped)
 
+        for index in range(1, 4):
+            idle = bank(index, [P, BANK])
+            nc.tensor.matmul_mx(
+                out=idle[:], lhsT=x_codes[0][:].bitcast(E4M3), lhsT_scale=x_plane[0][:],
+                rhs=r8[:, 0:BANK].bitcast(E4M3), rhs_scale=r8_plane[R8_ROW:, 0:BANK], start=True, stop=True,
+            )
+
         lists = [offsets[:, h * (HALF // 16) : (h + 1) * (HALF // 16)] for h in range(2)]
         got = {}
         got_plane = {}
@@ -180,7 +187,7 @@ def tile_list_mlat_resid_qf_mask_kernel(
         score_acc = {}
 
         def wv4_pass(n, h):
-            value_acc[n, h] = bank(2 * h + n % 2, [P, BANK])
+            value_acc[n, h] = bank(4 + n if (n >= 2 and h == 0) else 2 * h + n % 2, [P, BANK])
             nc.tensor.matmul_mx(
                 out=value_acc[n, h][:], lhsT=wv4[:, 2 * P * n : 2 * P * (n + 1)].bitcast(E2M1),
                 lhsT_scale=wv4_plane[:, P * n : P * (n + 1)],
@@ -199,7 +206,7 @@ def tile_list_mlat_resid_qf_mask_kernel(
             nc.sync.dma_start(out=out_1[n * P : (n + 1) * P, h * HALF : (h + 1) * HALF], in_=result[:])
 
         def score_passes(t, h):
-            score_acc[t, h] = bank(6 - 2 * t + h, [P, BANK])
+            score_acc[t, h] = bank(4 - 4 * t + h, [P, BANK])
             for a in (1, 0):
                 nc.tensor.matmul_mx(
                     out=score_acc[t, h][:], lhsT=qa_codes[t][:, P * a : P * (a + 1)].bitcast(E4M3),
@@ -218,6 +225,8 @@ def tile_list_mlat_resid_qf_mask_kernel(
         for h in range(2):
             for n in range(2):
                 wv4_pass(n, h)
+        for n in range(2, 4):
+            wv4_pass(n, 0)
         for h in range(2):
             for n in range(2):
                 wv8_pass(n, h)
@@ -228,10 +237,11 @@ def tile_list_mlat_resid_qf_mask_kernel(
             store_scores(0, h)
             quantize_wv8(2 + h)
         for h in range(2):
+            wv8_pass(2 + h, 0)
+            store_values(2 + h, 0, nc.scalar.copy)
             score_passes(1, h)
             store_scores(1, h)
         for n in range(2, 4):
-            for h in range(2):
-                wv4_pass(n, h)
-                wv8_pass(n, h)
-                store_values(n, h, nc.vector.tensor_copy if (n, h) == (3, 1) else nc.scalar.copy)
+            wv4_pass(n, 1)
+            wv8_pass(n, 1)
+            store_values(n, 1, nc.vector.tensor_copy if n == 3 else nc.scalar.copy)

@@ -26,9 +26,9 @@ TAB_ROW = (4, 0)
 R8_ROW = 8
 
 
-def load_scale_rows(queue, plane, first_row, rows):
+def load_scale_rows(queue, plane, first_row, rows, places=range(4)):
     by_place = rows.rearrange("(q r) n -> r q n", r=4)
-    for r in range(4):
+    for r in places:
         queue.dma_start(out=plane[first_row + r : P : 32, :].bitcast(I32), in_=by_place[r].bitcast(I32))
 
 
@@ -71,7 +71,7 @@ def tile_list_mlat_resid_qf_mask_kernel(
         wv8_rows = wv8.rearrange("(p j) n -> p j n", j=PACK)
 
         nc.gpsimd.memset(tab_plane[:].bitcast(I32), 0)
-        load_scale_rows(nc.gpsimd, tab_plane, TAB_ROW[0], tab_scales[0])
+        load_scale_rows(nc.gpsimd, tab_plane, TAB_ROW[0], tab_scales[0], range(0, 3))
         make_identity(nc, ident[:])
 
         nc.sync.dma_start(out=x_raw[:], in_=x.rearrange("(p j) m -> p j m", j=PACK))
@@ -83,9 +83,10 @@ def tile_list_mlat_resid_qf_mask_kernel(
         nc.sync.dma_start(out=r8[:].bitcast(I32), in_=r8_words[0].rearrange("p r i -> p (r i)").bitcast(I32))
         nc.sync.dma_start(out=tab[0][:, 0 : T // 2].bitcast(I32), in_=tab_rows[0][:, 0 : T // 2])
         load_scale_rows(nc.sync, tab_plane, TAB_ROW[1], tab_scales[1])
+        load_scale_rows(nc.sync, tab_plane, TAB_ROW[0], tab_scales[0], range(3, 4))
         nc.sync.dma_start(out=tab[0][:, T // 2 : T].bitcast(I32), in_=tab_rows[0][:, T // 2 : T])
-        nc.sync.dma_start(out=wv4[:].bitcast(I32), in_=wv4_words[0].bitcast(I32))
         nc.sync.dma_start(out=wv8_raw[0][:], in_=wv8_rows[:, :, 0 : N // 2])
+        nc.sync.dma_start(out=wv4[:].bitcast(I32), in_=wv4_words[0].bitcast(I32))
         load_scale_rows(nc.sync, wv4_plane, 0, wv4_scales[0])
         nc.sync.dma_start(out=wv8_raw[1][:], in_=wv8_rows[:, :, N // 2 : N])
         for t in range(2):
@@ -187,7 +188,7 @@ def tile_list_mlat_resid_qf_mask_kernel(
         score_acc = {}
 
         def wv4_pass(n, h):
-            value_acc[n, h] = bank(4 + n if (n >= 2 and h == 0) else 2 * h + n % 2, [P, BANK])
+            value_acc[n, h] = bank(2 * h + n if n < 2 else 4 + n - 2 * h, [P, BANK])
             nc.tensor.matmul_mx(
                 out=value_acc[n, h][:], lhsT=wv4[:, 2 * P * n : 2 * P * (n + 1)].bitcast(E2M1),
                 lhsT_scale=wv4_plane[:, P * n : P * (n + 1)],
@@ -206,7 +207,7 @@ def tile_list_mlat_resid_qf_mask_kernel(
             nc.sync.dma_start(out=out_1[n * P : (n + 1) * P, h * HALF : (h + 1) * HALF], in_=result[:])
 
         def score_passes(t, h):
-            score_acc[t, h] = bank(4 - 4 * t + h, [P, BANK])
+            score_acc[t, h] = bank(2 * t + h, [P, BANK])
             for a in (1, 0):
                 nc.tensor.matmul_mx(
                     out=score_acc[t, h][:], lhsT=qa_codes[t][:, P * a : P * (a + 1)].bitcast(E4M3),
@@ -225,9 +226,9 @@ def tile_list_mlat_resid_qf_mask_kernel(
         for h in range(2):
             for n in range(2):
                 wv4_pass(n, h)
-        for n in range(2, 4):
-            wv4_pass(n, 0)
         for h in range(2):
+            for n in range(2, 4):
+                wv4_pass(n, h)
             for n in range(2):
                 wv8_pass(n, h)
                 store_values(n, h, nc.scalar.copy)
@@ -236,12 +237,9 @@ def tile_list_mlat_resid_qf_mask_kernel(
             score_passes(0, h)
             store_scores(0, h)
             quantize_wv8(2 + h)
-        for h in range(2):
-            wv8_pass(2 + h, 0)
-            store_values(2 + h, 0, nc.scalar.copy)
-            score_passes(1, h)
-            store_scores(1, h)
-        for n in range(2, 4):
-            wv4_pass(n, 1)
-            wv8_pass(n, 1)
-            store_values(n, 1, nc.vector.tensor_copy if n == 3 else nc.scalar.copy)
+        for i in range(2):
+            for h in range(2):
+                wv8_pass(2 + i, h)
+                store_values(2 + i, h, nc.scalar.copy)
+            score_passes(1, i)
+            store_scores(1, i)

@@ -24,6 +24,7 @@ BANK = 512
 HALF = J // 2
 TAB_ROW = (4, 0)
 R8_ROW = 8
+ON_GPSIMD = 3
 
 
 def load_scale_rows(queue, plane, first_row, rows, places=range(4)):
@@ -45,10 +46,14 @@ def tile_list_mlat_resid_qf_mask_kernel(
     nc = tc.nc
     with ExitStack() as ctx:
         sb = ctx.enter_context(tc.tile_pool(name="sb", bufs=1))
+        laid = ctx.enter_context(tc.tile_pool(name="laid", bufs=1))
         ps = ctx.enter_context(tc.psum_pool(name="ps", bufs=1))
 
         def tile(name, shape, dtype, reuses=None):
             return sb.tile(shape, dtype, name=name, tag=reuses or name, align_bytes=64)
+
+        def laid_tile(name, shape, dtype, offset):
+            return laid.tile(shape, dtype, name=name, align_bytes=64, offset=offset)
 
         def bank(index, shape):
             return ps.tile(shape, F32, name="bank%d" % index, tag="bank%d" % index)
@@ -61,7 +66,7 @@ def tile_list_mlat_resid_qf_mask_kernel(
         x_raw = tile("x_raw", [P, PACK, M], F32)
         r8 = tile("r8", [P, R], U32)
         w4 = tile("w4", [P, 2 * R], U8)
-        tab = [tile("tab%d" % a, [P, T], U32) for a in range(2)]
+        tab = [laid_tile("tab0", [P, T], U32, 0), tile("tab1", [P, T], U32)]
         wv4 = tile("wv4", [P, 2 * N], U8)
         wv8_raw = [tile("wv8_raw%d" % g, [P, PACK, N // 2], F32) for g in range(2)]
         mask = [tile("mask%d" % t, [P, J], F32) for t in range(2)]
@@ -70,37 +75,37 @@ def tile_list_mlat_resid_qf_mask_kernel(
         tab_rows = [tab_words[a].rearrange("p t i -> p (t i)").bitcast(I32) for a in range(2)]
         wv8_rows = wv8.rearrange("(p j) n -> p j n", j=PACK)
 
-        nc.gpsimd.memset(tab_plane[:].bitcast(I32), 0)
-        load_scale_rows(nc.gpsimd, tab_plane, TAB_ROW[0], tab_scales[0], range(0, 3))
+        nc.vector.memset(tab_plane[:].bitcast(I32), 0)
         make_identity(nc, ident[:])
+        load_scale_rows(nc.gpsimd, tab_plane, TAB_ROW[0], tab_scales[0], range(ON_GPSIMD))
 
         nc.sync.dma_start(out=x_raw[:], in_=x.rearrange("(p j) m -> p j m", j=PACK))
         load_scale_rows(nc.sync, w4_plane, 0, w4_scales[0])
         nc.sync.dma_start(offsets[:], offs)
-        nc.sync.dma_start(out=w4[:].bitcast(I32), in_=w4_words[0].bitcast(I32))
         nc.sync.dma_start(out=tab[1][:].bitcast(I32), in_=tab_rows[1])
-        load_scale_rows(nc.sync, r8_plane, R8_ROW, r8_scales[0])
-        nc.sync.dma_start(out=r8[:].bitcast(I32), in_=r8_words[0].rearrange("p r i -> p (r i)").bitcast(I32))
-        nc.sync.dma_start(out=tab[0][:, 0 : T // 2].bitcast(I32), in_=tab_rows[0][:, 0 : T // 2])
+        nc.sync.dma_start(out=w4[:].bitcast(I32), in_=w4_words[0].bitcast(I32))
         load_scale_rows(nc.sync, tab_plane, TAB_ROW[1], tab_scales[1])
-        load_scale_rows(nc.sync, tab_plane, TAB_ROW[0], tab_scales[0], range(3, 4))
-        nc.sync.dma_start(out=tab[0][:, T // 2 : T].bitcast(I32), in_=tab_rows[0][:, T // 2 : T])
         nc.sync.dma_start(out=wv8_raw[0][:], in_=wv8_rows[:, :, 0 : N // 2])
+        nc.sync.dma_start(out=r8[:].bitcast(I32), in_=r8_words[0].rearrange("p r i -> p (r i)").bitcast(I32))
+        load_scale_rows(nc.sync, tab_plane, TAB_ROW[0], tab_scales[0], range(ON_GPSIMD, 4))
+        load_scale_rows(nc.sync, r8_plane, R8_ROW, r8_scales[0])
+        nc.sync.dma_start(out=tab[0][:].bitcast(I32), in_=tab_rows[0])
         nc.sync.dma_start(out=wv4[:].bitcast(I32), in_=wv4_words[0].bitcast(I32))
         load_scale_rows(nc.sync, wv4_plane, 0, wv4_scales[0])
         nc.sync.dma_start(out=wv8_raw[1][:], in_=wv8_rows[:, :, N // 2 : N])
         for t in range(2):
             nc.sync.dma_start(out=mask[t][:], in_=msk[t * P : (t + 1) * P, :])
 
+        def quantize(codes, plane, grouped):
+            nc.vector.quantize_mx(out=codes.bitcast(E4M3), scales=plane, in_=grouped)
+
         x_grouped = [tile("x_grouped%d" % t, [P, P, PACK], BF16) for t in range(2)]
         x_codes = [tile("x_codes%d" % t, [P, P], U32) for t in range(2)]
         x_plane = [tile("x_plane%d" % t, [P, P], U8) for t in range(2)]
         for t in range(2):
-            interleave(nc.vector.tensor_copy, x_grouped[t][:], x_raw[:, :, t * P : (t + 1) * P])
+            interleave(nc.scalar.copy, x_grouped[t][:], x_raw[:, :, t * P : (t + 1) * P])
         for t in range(2):
-            nc.vector.quantize_mx(
-                out=x_codes[t][:].bitcast(E4M3), scales=x_plane[t][:], in_=x_grouped[t][:].rearrange("p m j -> p (m j)")
-            )
+            quantize(x_codes[t][:], x_plane[t][:], x_grouped[t][:].rearrange("p m j -> p (m j)"))
 
         qa_acc = {}
         for t in range(2):
@@ -122,21 +127,28 @@ def tile_list_mlat_resid_qf_mask_kernel(
                 qa_rows[t, a] = tile("qa_rows%d%d" % (t, a), [P, 2, P, 2], BF16)
                 nc.scalar.copy(out=qa_rows[t, a][:], in_=qa_acc[t, a][:].rearrange("m (p u e) -> m u p e", u=2, e=2))
 
-        qa_grouped = []
+        early_grouped = tile("early_grouped", [P, 2 * P, PACK], BF16)
+        interleave(nc.scalar.copy, early_grouped[:], wv8_raw[0][:])
+
+        turned = []
         for t in range(2):
-            turned = bank(4 + t, [P, 2, 2, P])
+            turned.append(bank(4 + t, [P, 2, 2, P]))
             for a in range(2):
                 pairs = qa_rows[t, a][:].rearrange("m u p e -> m (u p e)").bitcast(F32)
                 for u in range(2):
-                    nc.tensor.transpose(turned[:, a, u, :], pairs[:, u * P : (u + 1) * P], ident[:])
-            grouped = tile("qa_grouped%d" % t, [P, 2 * P * PACK], BF16)
-            nc.scalar.copy(
-                out=grouped[:].bitcast(F32).rearrange("p (a m u) -> p a m u", a=2, u=2),
-                in_=turned[:].rearrange("p a u m -> p a m u"),
-            )
-            qa_grouped.append(grouped)
+                    nc.tensor.transpose(turned[t][:, a, u, :], pairs[:, u * P : (u + 1) * P], ident[:])
+        qa_grouped = {}
 
-        for index in range(1, 4):
+        def group_qa(t, reuses):
+            qa_grouped[t] = tile("qa_grouped%d" % t, [P, 2 * P * PACK], BF16, reuses)
+            nc.scalar.copy(
+                out=qa_grouped[t][:].bitcast(F32).rearrange("p (a m u) -> p a m u", a=2, u=2),
+                in_=turned[t][:].rearrange("p a u m -> p a m u"),
+            )
+
+        group_qa(0, None)
+
+        for index in (1, 2):
             idle = bank(index, [P, BANK])
             nc.tensor.matmul_mx(
                 out=idle[:], lhsT=x_codes[0][:].bitcast(E4M3), lhsT_scale=x_plane[0][:],
@@ -144,75 +156,61 @@ def tile_list_mlat_resid_qf_mask_kernel(
             )
 
         lists = [offsets[:, h * (HALF // 16) : (h + 1) * (HALF // 16)] for h in range(2)]
-        got = {}
-        got_plane = {}
-
-        def gather_words(a, h, reuses):
-            got[a, h] = tile("got%d%d" % (a, h), [P, HALF], U32, reuses)
-            nc.vector.tensor_copy(got[a, h][:], tab[a][:].indirect(lists[h]))
-
-        def gather_scales(h, reuses):
-            got_plane[h] = tile("got_plane%d" % h, [P, HALF], U8, reuses)
-            nc.vector.tensor_copy(got_plane[h][:], tab_plane[:].indirect(lists[h]))
-
-        gather_words(1, 0, None)
-        gather_words(1, 1, None)
-        gather_scales(0, "tab1")
-        gather_scales(1, None)
-        gather_words(0, 0, None)
-
-        wv8_grouped = [tile("wv8_grouped%d" % n, [P, P, PACK], BF16) for n in range(4)]
-        wv8_codes = [tile("wv8_codes%d" % n, [P, P], U32) for n in range(4)]
-        wv8_plane = [tile("wv8_plane%d" % n, [P, P], U8) for n in range(4)]
-
-        def cast_wv8(n):
-            interleave(nc.scalar.copy, wv8_grouped[n][:], wv8_raw[n // 2][:, :, (n % 2) * P : (n % 2 + 1) * P])
-
-        def quantize_wv8(n):
-            nc.vector.quantize_mx(
-                out=wv8_codes[n][:].bitcast(E4M3), scales=wv8_plane[n][:], in_=wv8_grouped[n][:].rearrange("p n j -> p (n j)")
-            )
-
-        for n in range(2):
-            cast_wv8(n)
-            quantize_wv8(n)
-        gather_words(0, 1, "wv8_grouped1")
-
-        qa_both = tile("qa_both", [P, 4 * P], U32, "tab0")
-        qa_codes = [qa_both[:, 2 * P * t : 2 * P * (t + 1)] for t in range(2)]
+        halves = [slice(h * HALF, (h + 1) * HALF) for h in range(2)]
+        got1 = tile("got1", [P, J], U32)
+        nc.vector.tensor_copy(got1[:], tab[1][:].indirect(offsets[:]))
+        plane_both = tile("got_plane", [P, J], U8, "tab1")
+        nc.vector.tensor_copy(plane_both[:], tab_plane[:].indirect(offsets[:]))
+        got = {(1, h): got1[:, halves[h]] for h in range(2)}
+        got_plane = [plane_both[:, halves[h]] for h in range(2)]
+        early_codes = tile("early_codes", [P, 2 * P], U32, "tab_plane")
+        early_plane = tile("early_plane", [P, 2 * P], U8)
+        quantize(early_codes[:], early_plane[:], early_grouped[:].rearrange("p n j -> p (n j)"))
+        for h in range(2):
+            got[0, h] = tile("got0%d" % h, [P, HALF], U32)[:]
+            nc.vector.tensor_copy(got[0, h], tab[0][:].indirect(lists[h]))
+        late_grouped = laid_tile("late_grouped", [P, 2 * P, PACK], BF16, 0)
+        late_codes = tile("late_codes", [P, 2 * P], U32)
+        late_plane = tile("late_plane", [P, 2 * P], U8)
+        qa_codes = [laid_tile("qa_codes0", [P, 2 * P], U32, 2 * (2 * P * PACK))[:], tile("qa_codes1", [P, 2 * P], U32)[:]]
         qa_plane = [tile("qa_plane%d" % t, [P, 2 * P], U8) for t in range(2)]
-        for t in range(2):
-            nc.vector.quantize_mx(out=qa_codes[t].bitcast(E4M3), scales=qa_plane[t][:], in_=qa_grouped[t][:])
+        interleave(nc.vector.tensor_copy, late_grouped[:], wv8_raw[1][:])
+        quantize(qa_codes[0], qa_plane[0][:], qa_grouped[0][:])
+        quantize(late_codes[:], late_plane[:], late_grouped[:].rearrange("p n j -> p (n j)"))
+        wv8_codes = [(early_codes, late_codes)[n // 2][:, (n % 2) * P : (n % 2 + 1) * P] for n in range(4)]
+        wv8_plane = [(early_plane, late_plane)[n // 2][:, (n % 2) * P : (n % 2 + 1) * P] for n in range(4)]
 
         value_acc = {}
         score_acc = {}
+        value_bank = {(0, 0): 0, (1, 0): 1, (0, 1): 2, (1, 1): 3, (2, 0): 6, (3, 0): 7, (2, 1): 4, (3, 1): 2}
+        score_bank = {(0, 0): 0, (0, 1): 1, (1, 0): 3, (1, 1): 5}
 
         def wv4_pass(n, h):
-            value_acc[n, h] = bank(2 * h + n if n < 2 else 4 + n - 2 * h, [P, BANK])
+            value_acc[n, h] = bank(value_bank[n, h], [P, BANK])
             nc.tensor.matmul_mx(
                 out=value_acc[n, h][:], lhsT=wv4[:, 2 * P * n : 2 * P * (n + 1)].bitcast(E2M1),
                 lhsT_scale=wv4_plane[:, P * n : P * (n + 1)],
-                rhs=got[1, h][:].bitcast(E4M3), rhs_scale=got_plane[h][TAB_ROW[1] :, :], start=True, stop=False,
+                rhs=got[1, h].bitcast(E4M3), rhs_scale=got_plane[h][TAB_ROW[1] :, :], start=True, stop=False,
             )
 
         def wv8_pass(n, h):
             nc.tensor.matmul_mx(
-                out=value_acc[n, h][:], lhsT=wv8_codes[n][:].bitcast(E4M3), lhsT_scale=wv8_plane[n][:],
-                rhs=got[0, h][:].bitcast(E4M3), rhs_scale=got_plane[h][TAB_ROW[0] :, :], start=False, stop=True,
+                out=value_acc[n, h][:], lhsT=wv8_codes[n].bitcast(E4M3), lhsT_scale=wv8_plane[n],
+                rhs=got[0, h].bitcast(E4M3), rhs_scale=got_plane[h][TAB_ROW[0] :, :], start=False, stop=True,
             )
 
-        def store_values(n, h, copy):
+        def store_values(n, h):
             result = tile("values%d%d" % (n, h), [P, HALF], F32)
-            copy(out=result[:], in_=value_acc[n, h][:])
+            nc.scalar.copy(out=result[:], in_=value_acc[n, h][:])
             nc.sync.dma_start(out=out_1[n * P : (n + 1) * P, h * HALF : (h + 1) * HALF], in_=result[:])
 
         def score_passes(t, h):
-            score_acc[t, h] = bank(2 * t + h, [P, BANK])
+            score_acc[t, h] = bank(score_bank[t, h], [P, BANK])
             for a in (1, 0):
                 nc.tensor.matmul_mx(
                     out=score_acc[t, h][:], lhsT=qa_codes[t][:, P * a : P * (a + 1)].bitcast(E4M3),
                     lhsT_scale=qa_plane[t][:, P * a : P * (a + 1)],
-                    rhs=got[a, h][:].bitcast(E4M3), rhs_scale=got_plane[h][TAB_ROW[a] :, :], start=(a == 1), stop=(a == 0),
+                    rhs=got[a, h].bitcast(E4M3), rhs_scale=got_plane[h][TAB_ROW[a] :, :], start=(a == 1), stop=(a == 0),
                 )
 
         def store_scores(t, h):
@@ -223,23 +221,25 @@ def tile_list_mlat_resid_qf_mask_kernel(
             )
             nc.sync.dma_start(out=out_0[t * P : (t + 1) * P, cols], in_=result[:])
 
+        for n, h in ((0, 0), (1, 0), (0, 1)):
+            wv4_pass(n, h)
         for h in range(2):
-            for n in range(2):
-                wv4_pass(n, h)
-        for h in range(2):
-            for n in range(2, 4):
-                wv4_pass(n, h)
             for n in range(2):
                 wv8_pass(n, h)
-                store_values(n, h, nc.scalar.copy)
-            cast_wv8(2 + h)
-        for h in range(2):
-            score_passes(0, h)
-            store_scores(0, h)
-            quantize_wv8(2 + h)
+                store_values(n, h)
+            if h == 0:
+                wv4_pass(1, 1)
+            wv4_pass(2 + h, 0)
+        group_qa(1, "tab_plane")
+        quantize(qa_codes[1], qa_plane[1][:], qa_grouped[1][:])
         for i in range(2):
-            for h in range(2):
-                wv8_pass(2 + i, h)
-                store_values(2 + i, h, nc.scalar.copy)
+            score_passes(0, i)
+            store_scores(0, i)
+            wv8_pass(2 + i, 0)
+            store_values(2 + i, 0)
+        for i in range(2):
+            wv4_pass(2 + i, 1)
+            wv8_pass(2 + i, 1)
+            store_values(2 + i, 1)
             score_passes(1, i)
             store_scores(1, i)

@@ -85,9 +85,9 @@ def tile_list_mlat_resid_qf_mask_kernel(
         nc.sync.dma_start(out=tab[1][:].bitcast(I32), in_=tab_rows[1])
         nc.sync.dma_start(out=w4[:].bitcast(I32), in_=w4_words[0].bitcast(I32))
         load_scale_rows(nc.sync, tab_plane, TAB_ROW[1], tab_scales[1])
-        nc.sync.dma_start(out=wv8_raw[0][:], in_=wv8_rows[:, :, 0 : N // 2])
-        nc.sync.dma_start(out=r8[:].bitcast(I32), in_=r8_words[0].rearrange("p r i -> p (r i)").bitcast(I32))
         load_scale_rows(nc.sync, tab_plane, TAB_ROW[0], tab_scales[0], range(ON_GPSIMD, 4))
+        nc.sync.dma_start(out=r8[:].bitcast(I32), in_=r8_words[0].rearrange("p r i -> p (r i)").bitcast(I32))
+        nc.sync.dma_start(out=wv8_raw[0][:], in_=wv8_rows[:, :, 0 : N // 2])
         load_scale_rows(nc.sync, r8_plane, R8_ROW, r8_scales[0])
         nc.sync.dma_start(out=tab[0][:].bitcast(I32), in_=tab_rows[0])
         nc.sync.dma_start(out=wv4[:].bitcast(I32), in_=wv4_words[0].bitcast(I32))

@@ -22,14 +22,12 @@ P = 128
 PACK = 4
 BANK = 512
 HALF = J // 2
-TAB_ROW = (4, 0)
 R8_ROW = 8
-ON_GPSIMD = 3
 
 
-def load_scale_rows(queue, plane, first_row, rows, places=range(4)):
+def load_scale_rows(queue, plane, first_row, rows):
     by_place = rows.rearrange("(q r) n -> r q n", r=4)
-    for r in places:
+    for r in range(4):
         queue.dma_start(out=plane[first_row + r : P : 32, :].bitcast(I32), in_=by_place[r].bitcast(I32))
 
 
@@ -61,40 +59,49 @@ def tile_list_mlat_resid_qf_mask_kernel(
         offsets = sb.tile([P, J // 16], U16, name="offsets")
         w4_plane = tile("w4_plane", [P, R], U8)
         r8_plane = tile("r8_plane", [P, R], U8)
-        tab_plane = tile("tab_plane", [P, T], U8)
-        wv4_plane = tile("wv4_plane", [P, N], U8)
         x_raw = tile("x_raw", [P, PACK, M], F32)
         r8 = tile("r8", [P, R], U32)
         w4 = tile("w4", [P, 2 * R], U8)
-        tab = [laid_tile("tab0", [P, T], U32, 0), tile("tab1", [P, T], U32)]
-        wv4 = tile("wv4", [P, 2 * N], U8)
-        wv8_raw = [tile("wv8_raw%d" % g, [P, PACK, N // 2], F32) for g in range(2)]
-        mask = [tile("mask%d" % t, [P, J], F32) for t in range(2)]
         ident = tile("ident", [P, P], F32)
+        scale_rows = laid_tile("scale_rows", [P, T], U8, 4 * T - 64)
+        tab = [tile("tab0", [P, T], U32), laid_tile("tab1", [P, T], U32, 0)]
+        wv4 = laid_tile("wv4", [P, 2 * N], U8, 4 * T)
+        wv4_plane = tile("wv4_plane", [P, N], U8)
+        wv8_raw = [tile("wv8_raw0", [P, PACK, N // 2], F32), laid_tile("wv8_raw1", [P, PACK, N // 2], F32, 4 * T + 3 * N)]
 
         tab_rows = [tab_words[a].rearrange("p t i -> p (t i)").bitcast(I32) for a in range(2)]
         wv8_rows = wv8.rearrange("(p j) n -> p j n", j=PACK)
 
-        nc.vector.memset(tab_plane[:].bitcast(I32), 0)
+        nc.vector.memset(scale_rows[32:64, :].bitcast(I32), 0)
+        nc.vector.memset(scale_rows[64:P, :].bitcast(I32), 0)
+        load_scale_rows(nc.gpsimd, wv4_plane, 0, wv4_scales[0])
         make_identity(nc, ident[:])
-        load_scale_rows(nc.gpsimd, tab_plane, TAB_ROW[0], tab_scales[0], range(ON_GPSIMD))
 
-        nc.sync.dma_start(out=x_raw[:], in_=x.rearrange("(p j) m -> p j m", j=PACK))
-        load_scale_rows(nc.sync, w4_plane, 0, w4_scales[0])
         nc.sync.dma_start(offsets[:], offs)
-        nc.sync.dma_start(out=tab[1][:].bitcast(I32), in_=tab_rows[1])
+        nc.sync.dma_start(out=scale_rows[0:32, :].bitcast(I32), in_=tab_scales.rearrange("a b t -> (a b) t").bitcast(I32))
+        load_scale_rows(nc.sync, w4_plane, 0, w4_scales[0])
+        nc.sync.dma_start(out=x_raw[:], in_=x.rearrange("(p j) m -> p j m", j=PACK))
         nc.sync.dma_start(out=w4[:].bitcast(I32), in_=w4_words[0].bitcast(I32))
-        load_scale_rows(nc.sync, tab_plane, TAB_ROW[1], tab_scales[1])
-        load_scale_rows(nc.sync, tab_plane, TAB_ROW[0], tab_scales[0], range(ON_GPSIMD, 4))
         nc.sync.dma_start(out=r8[:].bitcast(I32), in_=r8_words[0].rearrange("p r i -> p (r i)").bitcast(I32))
-        nc.sync.dma_start(out=wv8_raw[0][:], in_=wv8_rows[:, :, 0 : N // 2])
         load_scale_rows(nc.sync, r8_plane, R8_ROW, r8_scales[0])
+        nc.sync.dma_start(out=wv8_raw[0][:], in_=wv8_rows[:, :, 0 : N // 2])
         nc.sync.dma_start(out=tab[0][:].bitcast(I32), in_=tab_rows[0])
+
+        got_rows = tile("got_rows", [P, J], U8)
+        nc.vector.tensor_copy(got_rows[:], scale_rows[:].indirect(offsets[:]))
+        tab_plane = [tile("tab_plane%d" % a, [P, J], U8) for a in range(2)]
+
+        def move_scale_rows(a):
+            for r in range(4):
+                nc.sync.dma_start(
+                    out=tab_plane[a][r:P:32, :].bitcast(I32), in_=got_rows[16 * a + r : 16 * (a + 1) : 4, :].bitcast(I32)
+                )
+
+        move_scale_rows(0)
+        nc.sync.dma_start(out=tab[1][:].bitcast(I32), in_=tab_rows[1])
         nc.sync.dma_start(out=wv4[:].bitcast(I32), in_=wv4_words[0].bitcast(I32))
-        load_scale_rows(nc.sync, wv4_plane, 0, wv4_scales[0])
+        move_scale_rows(1)
         nc.sync.dma_start(out=wv8_raw[1][:], in_=wv8_rows[:, :, N // 2 : N])
-        for t in range(2):
-            nc.sync.dma_start(out=mask[t][:], in_=msk[t * P : (t + 1) * P, :])
 
         def quantize(codes, plane, grouped):
             nc.vector.quantize_mx(out=codes.bitcast(E4M3), scales=plane, in_=grouped)
@@ -106,6 +113,10 @@ def tile_list_mlat_resid_qf_mask_kernel(
             interleave(nc.scalar.copy, x_grouped[t][:], x_raw[:, :, t * P : (t + 1) * P])
         for t in range(2):
             quantize(x_codes[t][:], x_plane[t][:], x_grouped[t][:].rearrange("p m j -> p (m j)"))
+
+        lists = [offsets[:, h * (HALF // 16) : (h + 1) * (HALF // 16)] for h in range(2)]
+        halves = [slice(h * HALF, (h + 1) * HALF) for h in range(2)]
+        got = {}
 
         qa_acc = {}
         for t in range(2):
@@ -124,122 +135,136 @@ def tile_list_mlat_resid_qf_mask_kernel(
                     rhs=r8[:, BANK * a : BANK * (a + 1)].bitcast(E4M3), rhs_scale=r8_plane[R8_ROW:, BANK * a : BANK * (a + 1)],
                     start=False, stop=True,
                 )
-                qa_rows[t, a] = tile("qa_rows%d%d" % (t, a), [P, 2, P, 2], BF16)
-                nc.scalar.copy(out=qa_rows[t, a][:], in_=qa_acc[t, a][:].rearrange("m (p u e) -> m u p e", u=2, e=2))
-
-        early_grouped = tile("early_grouped", [P, 2 * P, PACK], BF16)
-        interleave(nc.scalar.copy, early_grouped[:], wv8_raw[0][:])
-
-        turned = []
+        mask = [tile("mask%d" % t, [P, J], F32, ("w4", "r8")[t]) for t in range(2)]
         for t in range(2):
-            turned.append(bank(4 + t, [P, 2, 2, P]))
+            nc.sync.dma_start(out=mask[t][:], in_=msk[t * P : (t + 1) * P, :])
+
+        def empty_qa(t, a, copy):
+            qa_rows[t, a] = tile("qa_rows%d%d" % (t, a), [P, 2, P, 2], BF16)
+            copy(out=qa_rows[t, a][:], in_=qa_acc[t, a][:].rearrange("m (p u e) -> m u p e", u=2, e=2))
+
+        share_raw = [wv8_raw[0][:], wv8_raw[1][:, :, 0:P], wv8_raw[1][:, :, P : 2 * P]]
+        share_width = (2 * P, P, P)
+        share_grouped = [
+            tile("wv8_grouped0", [P, 2 * P, PACK], BF16),
+            tile("wv8_grouped1", [P, P, PACK], BF16),
+            laid_tile("wv8_grouped2", [P, P, PACK], BF16, 0),
+        ]
+        share_codes = [
+            tile("wv8_codes0", [P, 2 * P], U32),
+            laid_tile("wv8_codes1", [P, P], U32, 1024),
+            tile("wv8_codes2", [P, P], U32),
+        ]
+        share_plane = [tile("wv8_plane%d" % g, [P, share_width[g]], U8) for g in range(3)]
+        wv8_codes = [share_codes[0][:, 0:P], share_codes[0][:, P : 2 * P], share_codes[1][:], share_codes[2][:]]
+        wv8_plane = [share_plane[0][:, 0:P], share_plane[0][:, P : 2 * P], share_plane[1][:], share_plane[2][:]]
+
+        def quantize_wv8(g):
+            quantize(share_codes[g][:], share_plane[g][:], share_grouped[g][:].rearrange("p n j -> p (n j)"))
+
+        turned = {}
+        qa_grouped = {}
+        qa_codes = [laid_tile("qa_codes0", [P, 2 * P], U32, 2048), tile("qa_codes1", [P, 2 * P], U32, "w4")]
+        qa_plane = [tile("qa_plane%d" % t, [P, 2 * P], U8) for t in range(2)]
+
+        def turn_qa(t):
+            turned[t] = bank(2 * t, [P, 2, 2, P])
             for a in range(2):
                 pairs = qa_rows[t, a][:].rearrange("m u p e -> m (u p e)").bitcast(F32)
                 for u in range(2):
                     nc.tensor.transpose(turned[t][:, a, u, :], pairs[:, u * P : (u + 1) * P], ident[:])
-        qa_grouped = {}
-
-        def group_qa(t, reuses):
-            qa_grouped[t] = tile("qa_grouped%d" % t, [P, 2 * P * PACK], BF16, reuses)
+            qa_grouped[t] = tile("qa_grouped%d" % t, [P, 2 * P * PACK], BF16)
             nc.scalar.copy(
                 out=qa_grouped[t][:].bitcast(F32).rearrange("p (a m u) -> p a m u", a=2, u=2),
                 in_=turned[t][:].rearrange("p a u m -> p a m u"),
             )
 
-        group_qa(0, None)
-
-        for index in (1, 2):
-            idle = bank(index, [P, BANK])
-            nc.tensor.matmul_mx(
-                out=idle[:], lhsT=x_codes[0][:].bitcast(E4M3), lhsT_scale=x_plane[0][:],
-                rhs=r8[:, 0:BANK].bitcast(E4M3), rhs_scale=r8_plane[R8_ROW:, 0:BANK], start=True, stop=True,
-            )
-
-        lists = [offsets[:, h * (HALF // 16) : (h + 1) * (HALF // 16)] for h in range(2)]
-        halves = [slice(h * HALF, (h + 1) * HALF) for h in range(2)]
-        got1 = tile("got1", [P, J], U32)
-        nc.vector.tensor_copy(got1[:], tab[1][:].indirect(offsets[:]))
-        plane_both = tile("got_plane", [P, J], U8, "tab1")
-        nc.vector.tensor_copy(plane_both[:], tab_plane[:].indirect(offsets[:]))
-        got = {(1, h): got1[:, halves[h]] for h in range(2)}
-        got_plane = [plane_both[:, halves[h]] for h in range(2)]
-        early_codes = tile("early_codes", [P, 2 * P], U32, "tab_plane")
-        early_plane = tile("early_plane", [P, 2 * P], U8)
-        quantize(early_codes[:], early_plane[:], early_grouped[:].rearrange("p n j -> p (n j)"))
-        for h in range(2):
-            got[0, h] = tile("got0%d" % h, [P, HALF], U32)[:]
-            nc.vector.tensor_copy(got[0, h], tab[0][:].indirect(lists[h]))
-        late_grouped = laid_tile("late_grouped", [P, 2 * P, PACK], BF16, 0)
-        late_codes = tile("late_codes", [P, 2 * P], U32)
-        late_plane = tile("late_plane", [P, 2 * P], U8)
-        qa_codes = [laid_tile("qa_codes0", [P, 2 * P], U32, 2 * (2 * P * PACK))[:], tile("qa_codes1", [P, 2 * P], U32)[:]]
-        qa_plane = [tile("qa_plane%d" % t, [P, 2 * P], U8) for t in range(2)]
-        interleave(nc.vector.tensor_copy, late_grouped[:], wv8_raw[1][:])
-        quantize(qa_codes[0], qa_plane[0][:], qa_grouped[0][:])
-        quantize(late_codes[:], late_plane[:], late_grouped[:].rearrange("p n j -> p (n j)"))
-        wv8_codes = [(early_codes, late_codes)[n // 2][:, (n % 2) * P : (n % 2 + 1) * P] for n in range(4)]
-        wv8_plane = [(early_plane, late_plane)[n // 2][:, (n % 2) * P : (n % 2 + 1) * P] for n in range(4)]
-
         value_acc = {}
         score_acc = {}
-        value_bank = {(0, 0): 0, (1, 0): 1, (0, 1): 2, (1, 1): 3, (2, 0): 6, (3, 0): 7, (2, 1): 4, (3, 1): 2}
-        score_bank = {(0, 0): 0, (0, 1): 1, (1, 0): 3, (1, 1): 5}
+        score_bank = {(0, 0): 4, (0, 1): 5, (1, 0): 6, (1, 1): 7}
+        value_bank = {(0, 0): 4, (1, 0): 5, (0, 1): 6, (1, 1): 7, (2, 0): 1, (3, 0): 3, (2, 1): 0, (3, 1): 2}
 
-        def wv4_pass(n, h):
-            value_acc[n, h] = bank(value_bank[n, h], [P, BANK])
+        def wv4_pass(n, h, opens):
+            if opens:
+                value_acc[n, h] = bank(value_bank[n, h], [P, BANK])
             nc.tensor.matmul_mx(
                 out=value_acc[n, h][:], lhsT=wv4[:, 2 * P * n : 2 * P * (n + 1)].bitcast(E2M1),
                 lhsT_scale=wv4_plane[:, P * n : P * (n + 1)],
-                rhs=got[1, h].bitcast(E4M3), rhs_scale=got_plane[h][TAB_ROW[1] :, :], start=True, stop=False,
+                rhs=got[1, h].bitcast(E4M3), rhs_scale=tab_plane[1][:, halves[h]], start=opens, stop=not opens,
             )
 
-        def wv8_pass(n, h):
+        def wv8_pass(n, h, opens):
+            if opens:
+                value_acc[n, h] = bank(value_bank[n, h], [P, BANK])
             nc.tensor.matmul_mx(
                 out=value_acc[n, h][:], lhsT=wv8_codes[n].bitcast(E4M3), lhsT_scale=wv8_plane[n],
-                rhs=got[0, h].bitcast(E4M3), rhs_scale=got_plane[h][TAB_ROW[0] :, :], start=False, stop=True,
+                rhs=got[0, h].bitcast(E4M3), rhs_scale=tab_plane[0][:, halves[h]], start=opens, stop=not opens,
             )
 
-        def store_values(n, h):
+        def store_values(n, h, copy):
             result = tile("values%d%d" % (n, h), [P, HALF], F32)
-            nc.scalar.copy(out=result[:], in_=value_acc[n, h][:])
-            nc.sync.dma_start(out=out_1[n * P : (n + 1) * P, h * HALF : (h + 1) * HALF], in_=result[:])
+            copy(out=result[:], in_=value_acc[n, h][:])
+            nc.sync.dma_start(out=out_1[n * P : (n + 1) * P, halves[h]], in_=result[:])
 
-        def score_passes(t, h):
-            score_acc[t, h] = bank(score_bank[t, h], [P, BANK])
-            for a in (1, 0):
-                nc.tensor.matmul_mx(
-                    out=score_acc[t, h][:], lhsT=qa_codes[t][:, P * a : P * (a + 1)].bitcast(E4M3),
-                    lhsT_scale=qa_plane[t][:, P * a : P * (a + 1)],
-                    rhs=got[a, h].bitcast(E4M3), rhs_scale=got_plane[h][TAB_ROW[a] :, :], start=(a == 1), stop=(a == 0),
-                )
+        def store_value_rows(n, copies):
+            result = tile("values%d" % n, [P, J], F32)
+            for h in range(2):
+                wv8_pass(n, h, False)
+                copies[h](out=result[:, halves[h]], in_=value_acc[n, h][:])
+            nc.sync.dma_start(out=out_1[n * P : (n + 1) * P, :], in_=result[:])
 
-        def store_scores(t, h):
-            cols = slice(h * HALF, (h + 1) * HALF)
-            result = tile("scores%d%d" % (t, h), [P, HALF], F32)
-            nc.vector.scalar_tensor_tensor(
-                out=result[:], in0=score_acc[t, h][:], scalar=SCORE_SCALE, in1=mask[t][:, cols], op0=MULT, op1=ADD
+        def score_pass(t, h, a):
+            if a == 0:
+                score_acc[t, h] = bank(score_bank[t, h], [P, BANK])
+            nc.tensor.matmul_mx(
+                out=score_acc[t, h][:], lhsT=qa_codes[t][:, P * a : P * (a + 1)].bitcast(E4M3),
+                lhsT_scale=qa_plane[t][:, P * a : P * (a + 1)],
+                rhs=got[a, h].bitcast(E4M3), rhs_scale=tab_plane[a][:, halves[h]], start=(a == 0), stop=(a == 1),
             )
-            nc.sync.dma_start(out=out_0[t * P : (t + 1) * P, cols], in_=result[:])
 
-        for n, h in ((0, 0), (1, 0), (0, 1)):
-            wv4_pass(n, h)
+        def store_scores(t):
+            result = tile("scores%d" % t, [P, J], F32)
+            for h in range(2):
+                score_pass(t, h, 0)
+                score_pass(t, h, 1)
+                nc.vector.scalar_tensor_tensor(
+                    out=result[:, halves[h]], in0=score_acc[t, h][:], scalar=SCORE_SCALE, in1=mask[t][:, halves[h]], op0=MULT, op1=ADD
+                )
+            nc.sync.dma_start(out=out_0[t * P : (t + 1) * P, :], in_=result[:])
+
+        def gather_half(a, h):
+            got[a, h] = tile("got%d%d" % (a, h), [P, HALF], U32)[:]
+            nc.vector.tensor_copy(got[a, h], tab[a][:].indirect(lists[h]))
+
+        interleave(nc.vector.tensor_copy, share_grouped[0][:], share_raw[0])
+        quantize_wv8(0)
+        gather_half(0, 0)
+        gather_half(0, 1)
+        for t in range(2):
+            for a in range(2):
+                empty_qa(t, a, nc.scalar.copy)
+        turn_qa(0)
+        turn_qa(1)
         for h in range(2):
             for n in range(2):
-                wv8_pass(n, h)
-                store_values(n, h)
+                wv8_pass(n, h, True)
+        gather_half(1, 0)
+        gather_half(1, 1)
+        interleave(nc.scalar.copy, share_grouped[1][:], share_raw[1])
+        quantize(qa_codes[0][:], qa_plane[0][:], qa_grouped[0][:])
+        quantize_wv8(1)
+        interleave(nc.vector.tensor_copy, share_grouped[2][:], share_raw[2])
+        for h in range(2):
+            for n in range(2):
+                wv4_pass(n, h, False)
+                store_values(n, h, nc.scalar.copy)
             if h == 0:
-                wv4_pass(1, 1)
-            wv4_pass(2 + h, 0)
-        group_qa(1, "tab_plane")
-        quantize(qa_codes[1], qa_plane[1][:], qa_grouped[1][:])
-        for i in range(2):
-            score_passes(0, i)
-            store_scores(0, i)
-            wv8_pass(2 + i, 0)
-            store_values(2 + i, 0)
-        for i in range(2):
-            wv4_pass(2 + i, 1)
-            wv8_pass(2 + i, 1)
-            store_values(2 + i, 1)
-            score_passes(1, i)
-            store_scores(1, i)
+                for n in range(2, 4):
+                    wv4_pass(n, 0, True)
+        quantize_wv8(2)
+        store_scores(0)
+        quantize(qa_codes[1][:], qa_plane[1][:], qa_grouped[1][:])
+        for n in range(2, 4):
+            wv4_pass(n, 1, True)
+            store_value_rows(n, (nc.scalar.copy, nc.scalar.copy))
+        store_scores(1)

@@ -25,9 +25,9 @@ HALF = J // 2
 R8_ROW = 8
 
 
-def load_scale_rows(queue, plane, first_row, rows):
+def load_scale_rows(queue, plane, first_row, rows, places=range(4)):
     by_place = rows.rearrange("(q r) n -> r q n", r=4)
-    for r in range(4):
+    for r in places:
         queue.dma_start(out=plane[first_row + r : P : 32, :].bitcast(I32), in_=by_place[r].bitcast(I32))
 
 
@@ -74,18 +74,19 @@ def tile_list_mlat_resid_qf_mask_kernel(
 
         nc.vector.memset(scale_rows[32:64, :].bitcast(I32), 0)
         nc.vector.memset(scale_rows[64:P, :].bitcast(I32), 0)
+        load_scale_rows(nc.gpsimd, w4_plane, 0, w4_scales[0], range(1))
         load_scale_rows(nc.gpsimd, wv4_plane, 0, wv4_scales[0])
         make_identity(nc, ident[:])
 
         nc.sync.dma_start(offsets[:], offs)
         nc.sync.dma_start(out=scale_rows[0:32, :].bitcast(I32), in_=tab_scales.rearrange("a b t -> (a b) t").bitcast(I32))
-        load_scale_rows(nc.sync, w4_plane, 0, w4_scales[0])
         nc.sync.dma_start(out=x_raw[:], in_=x.rearrange("(p j) m -> p j m", j=PACK))
+        load_scale_rows(nc.sync, w4_plane, 0, w4_scales[0], range(1, 4))
         nc.sync.dma_start(out=w4[:].bitcast(I32), in_=w4_words[0].bitcast(I32))
-        nc.sync.dma_start(out=r8[:].bitcast(I32), in_=r8_words[0].rearrange("p r i -> p (r i)").bitcast(I32))
-        load_scale_rows(nc.sync, r8_plane, R8_ROW, r8_scales[0])
-        nc.sync.dma_start(out=wv8_raw[0][:], in_=wv8_rows[:, :, 0 : N // 2])
         nc.sync.dma_start(out=tab[0][:].bitcast(I32), in_=tab_rows[0])
+        load_scale_rows(nc.sync, r8_plane, R8_ROW, r8_scales[0])
+        nc.sync.dma_start(out=r8[:].bitcast(I32), in_=r8_words[0].rearrange("p r i -> p (r i)").bitcast(I32))
+        nc.sync.dma_start(out=wv8_raw[0][:], in_=wv8_rows[:, :, 0 : N // 2])
 
         got_rows = tile("got_rows", [P, J], U8)
         nc.vector.tensor_copy(got_rows[:], scale_rows[:].indirect(offsets[:]))
@@ -236,10 +237,10 @@ def tile_list_mlat_resid_qf_mask_kernel(
             got[a, h] = tile("got%d%d" % (a, h), [P, HALF], U32)[:]
             nc.vector.tensor_copy(got[a, h], tab[a][:].indirect(lists[h]))
 
-        interleave(nc.vector.tensor_copy, share_grouped[0][:], share_raw[0])
-        quantize_wv8(0)
         gather_half(0, 0)
         gather_half(0, 1)
+        interleave(nc.vector.tensor_copy, share_grouped[0][:], share_raw[0])
+        quantize_wv8(0)
         for t in range(2):
             for a in range(2):
                 empty_qa(t, a, nc.scalar.copy)

@@ -74,17 +74,17 @@ def tile_list_mlat_resid_qf_mask_kernel(
 
         nc.vector.memset(scale_rows[32:64, :].bitcast(I32), 0)
         nc.vector.memset(scale_rows[64:P, :].bitcast(I32), 0)
-        load_scale_rows(nc.gpsimd, w4_plane, 0, w4_scales[0], range(1))
         load_scale_rows(nc.gpsimd, wv4_plane, 0, wv4_scales[0])
         make_identity(nc, ident[:])
 
         nc.sync.dma_start(offsets[:], offs)
         nc.sync.dma_start(out=scale_rows[0:32, :].bitcast(I32), in_=tab_scales.rearrange("a b t -> (a b) t").bitcast(I32))
         nc.sync.dma_start(out=x_raw[:], in_=x.rearrange("(p j) m -> p j m", j=PACK))
-        load_scale_rows(nc.sync, w4_plane, 0, w4_scales[0], range(1, 4))
+        load_scale_rows(nc.sync, w4_plane, 0, w4_scales[0])
         nc.sync.dma_start(out=w4[:].bitcast(I32), in_=w4_words[0].bitcast(I32))
+        load_scale_rows(nc.sync, r8_plane, R8_ROW, r8_scales[0], range(1))
         nc.sync.dma_start(out=tab[0][:].bitcast(I32), in_=tab_rows[0])
-        load_scale_rows(nc.sync, r8_plane, R8_ROW, r8_scales[0])
+        load_scale_rows(nc.sync, r8_plane, R8_ROW, r8_scales[0], range(1, 4))
         nc.sync.dma_start(out=r8[:].bitcast(I32), in_=r8_words[0].rearrange("p r i -> p (r i)").bitcast(I32))
         nc.sync.dma_start(out=wv8_raw[0][:], in_=wv8_rows[:, :, 0 : N // 2])
 
@@ -144,24 +144,14 @@ def tile_list_mlat_resid_qf_mask_kernel(
             qa_rows[t, a] = tile("qa_rows%d%d" % (t, a), [P, 2, P, 2], BF16)
             copy(out=qa_rows[t, a][:], in_=qa_acc[t, a][:].rearrange("m (p u e) -> m u p e", u=2, e=2))
 
-        share_raw = [wv8_raw[0][:], wv8_raw[1][:, :, 0:P], wv8_raw[1][:, :, P : 2 * P]]
-        share_width = (2 * P, P, P)
-        share_grouped = [
-            tile("wv8_grouped0", [P, 2 * P, PACK], BF16),
-            tile("wv8_grouped1", [P, P, PACK], BF16),
-            laid_tile("wv8_grouped2", [P, P, PACK], BF16, 0),
-        ]
-        share_codes = [
-            tile("wv8_codes0", [P, 2 * P], U32),
-            laid_tile("wv8_codes1", [P, P], U32, 1024),
-            tile("wv8_codes2", [P, P], U32),
-        ]
-        share_plane = [tile("wv8_plane%d" % g, [P, share_width[g]], U8) for g in range(3)]
-        wv8_codes = [share_codes[0][:, 0:P], share_codes[0][:, P : 2 * P], share_codes[1][:], share_codes[2][:]]
-        wv8_plane = [share_plane[0][:, 0:P], share_plane[0][:, P : 2 * P], share_plane[1][:], share_plane[2][:]]
+        wv8_grouped = [tile("wv8_grouped0", [P, 2 * P, PACK], BF16), laid_tile("wv8_grouped1", [P, 2 * P, PACK], BF16, 0)]
+        half_codes = [tile("wv8_codes%d" % g, [P, 2 * P], U32) for g in range(2)]
+        half_plane = [tile("wv8_plane%d" % g, [P, 2 * P], U8) for g in range(2)]
+        wv8_codes = [half_codes[n // 2][:, (n % 2) * P : (n % 2 + 1) * P] for n in range(4)]
+        wv8_plane = [half_plane[n // 2][:, (n % 2) * P : (n % 2 + 1) * P] for n in range(4)]
 
         def quantize_wv8(g):
-            quantize(share_codes[g][:], share_plane[g][:], share_grouped[g][:].rearrange("p n j -> p (n j)"))
+            quantize(half_codes[g][:], half_plane[g][:], wv8_grouped[g][:].rearrange("p n j -> p (n j)"))
 
         turned = {}
         qa_grouped = {}
@@ -169,7 +159,7 @@ def tile_list_mlat_resid_qf_mask_kernel(
         qa_plane = [tile("qa_plane%d" % t, [P, 2 * P], U8) for t in range(2)]
 
         def turn_qa(t):
-            turned[t] = bank(2 * t, [P, 2, 2, P])
+            turned[t] = bank(4 * t, [P, 2, 2, P])
             for a in range(2):
                 pairs = qa_rows[t, a][:].rearrange("m u p e -> m (u p e)").bitcast(F32)
                 for u in range(2):
@@ -182,8 +172,8 @@ def tile_list_mlat_resid_qf_mask_kernel(
 
         value_acc = {}
         score_acc = {}
-        score_bank = {(0, 0): 4, (0, 1): 5, (1, 0): 6, (1, 1): 7}
-        value_bank = {(0, 0): 4, (1, 0): 5, (0, 1): 6, (1, 1): 7, (2, 0): 1, (3, 0): 3, (2, 1): 0, (3, 1): 2}
+        score_bank = {(0, 0): 1, (0, 1): 2, (1, 0): 7, (1, 1): 4}
+        value_bank = {(0, 0): 1, (1, 0): 2, (0, 1): 3, (1, 1): 0, (2, 0): 5, (3, 0): 6, (2, 1): 3, (3, 1): 0}
 
         def wv4_pass(n, h, opens):
             if opens:
@@ -223,7 +213,7 @@ def tile_list_mlat_resid_qf_mask_kernel(
                 rhs=got[a, h].bitcast(E4M3), rhs_scale=tab_plane[a][:, halves[h]], start=(a == 0), stop=(a == 1),
             )
 
-        def store_scores(t):
+        def store_scores(t, whole):
             result = tile("scores%d" % t, [P, J], F32)
             for h in range(2):
                 score_pass(t, h, 0)
@@ -231,7 +221,10 @@ def tile_list_mlat_resid_qf_mask_kernel(
                 nc.vector.scalar_tensor_tensor(
                     out=result[:, halves[h]], in0=score_acc[t, h][:], scalar=SCORE_SCALE, in1=mask[t][:, halves[h]], op0=MULT, op1=ADD
                 )
-            nc.sync.dma_start(out=out_0[t * P : (t + 1) * P, :], in_=result[:])
+                if not whole:
+                    nc.sync.dma_start(out=out_0[t * P : (t + 1) * P, halves[h]], in_=result[:, halves[h]])
+            if whole:
+                nc.sync.dma_start(out=out_0[t * P : (t + 1) * P, :], in_=result[:])
 
         def gather_half(a, h):
             got[a, h] = tile("got%d%d" % (a, h), [P, HALF], U32)[:]
@@ -239,22 +232,21 @@ def tile_list_mlat_resid_qf_mask_kernel(
 
         gather_half(0, 0)
         gather_half(0, 1)
-        interleave(nc.vector.tensor_copy, share_grouped[0][:], share_raw[0])
+        interleave(nc.vector.tensor_copy, wv8_grouped[0][:], wv8_raw[0][:])
         quantize_wv8(0)
         for t in range(2):
             for a in range(2):
                 empty_qa(t, a, nc.scalar.copy)
         turn_qa(0)
+        for n in range(2):
+            wv8_pass(n, 0, True)
         turn_qa(1)
-        for h in range(2):
-            for n in range(2):
-                wv8_pass(n, h, True)
+        for n in range(2):
+            wv8_pass(n, 1, True)
         gather_half(1, 0)
         gather_half(1, 1)
-        interleave(nc.scalar.copy, share_grouped[1][:], share_raw[1])
         quantize(qa_codes[0][:], qa_plane[0][:], qa_grouped[0][:])
-        quantize_wv8(1)
-        interleave(nc.vector.tensor_copy, share_grouped[2][:], share_raw[2])
+        interleave(nc.vector.tensor_copy, wv8_grouped[1][:], wv8_raw[1][:])
         for h in range(2):
             for n in range(2):
                 wv4_pass(n, h, False)
@@ -262,10 +254,10 @@ def tile_list_mlat_resid_qf_mask_kernel(
             if h == 0:
                 for n in range(2, 4):
                     wv4_pass(n, 0, True)
-        quantize_wv8(2)
-        store_scores(0)
+        quantize_wv8(1)
+        store_scores(0, False)
         quantize(qa_codes[1][:], qa_plane[1][:], qa_grouped[1][:])
         for n in range(2, 4):
             wv4_pass(n, 1, True)
             store_value_rows(n, (nc.scalar.copy, nc.scalar.copy))
-        store_scores(1)
+        store_scores(1, True)

@@ -22,6 +22,7 @@ P = 128
 PACK = 4
 BANK = 512
 HALF = J // 2
+TAB_ROW = (4, 0)
 R8_ROW = 8
 
 
@@ -95,7 +96,7 @@ def tile_list_mlat_resid_qf_mask_kernel(
         def move_scale_rows(a):
             for r in range(4):
                 nc.sync.dma_start(
-                    out=tab_plane[a][r:P:32, :].bitcast(I32), in_=got_rows[16 * a + r : 16 * (a + 1) : 4, :].bitcast(I32)
+                    out=tab_plane[a][TAB_ROW[a] + r : P : 32, :].bitcast(I32), in_=got_rows[16 * a + r : 16 * (a + 1) : 4, :].bitcast(I32)
                 )
 
         move_scale_rows(0)
@@ -189,7 +190,7 @@ def tile_list_mlat_resid_qf_mask_kernel(
                 value_acc[n, h] = bank(value_bank[n, h], [P, BANK])
             nc.tensor.matmul_mx(
                 out=value_acc[n, h][:], lhsT=wv8_codes[n].bitcast(E4M3), lhsT_scale=wv8_plane[n],
-                rhs=got[0, h].bitcast(E4M3), rhs_scale=tab_plane[0][:, halves[h]], start=opens, stop=not opens,
+                rhs=got[0, h].bitcast(E4M3), rhs_scale=tab_plane[0][TAB_ROW[0] :, halves[h]], start=opens, stop=not opens,
             )
 
         def store_values(n, h, copy):
@@ -210,7 +211,7 @@ def tile_list_mlat_resid_qf_mask_kernel(
             nc.tensor.matmul_mx(
                 out=score_acc[t, h][:], lhsT=qa_codes[t][:, P * a : P * (a + 1)].bitcast(E4M3),
                 lhsT_scale=qa_plane[t][:, P * a : P * (a + 1)],
-                rhs=got[a, h].bitcast(E4M3), rhs_scale=tab_plane[a][:, halves[h]], start=(a == 0), stop=(a == 1),
+                rhs=got[a, h].bitcast(E4M3), rhs_scale=tab_plane[a][TAB_ROW[a] :, halves[h]], start=(a == 0), stop=(a == 1),
             )
 
         def store_scores(t, whole):

@@ -64,18 +64,16 @@ def tile_list_mlat_resid_qf_mask_kernel(
         r8 = tile("r8", [P, R], U32)
         w4 = tile("w4", [P, 2 * R], U8)
         ident = tile("ident", [P, P], F32)
-        scale_rows = laid_tile("scale_rows", [P, T], U8, 4 * T - 64)
+        scale_rows = tile("scale_rows", [P, T], U8)
         tab = [tile("tab0", [P, T], U32), laid_tile("tab1", [P, T], U32, 0)]
-        wv4 = laid_tile("wv4", [P, 2 * N], U8, 4 * T)
-        wv4_plane = tile("wv4_plane", [P, N], U8)
-        wv8_raw = [tile("wv8_raw0", [P, PACK, N // 2], F32), laid_tile("wv8_raw1", [P, PACK, N // 2], F32, 4 * T + 3 * N)]
+        wv8_raw = [tile("wv8_raw0", [P, PACK, N // 2], F32)]
 
         tab_rows = [tab_words[a].rearrange("p t i -> p (t i)").bitcast(I32) for a in range(2)]
         wv8_rows = wv8.rearrange("(p j) n -> p j n", j=PACK)
 
         nc.vector.memset(scale_rows[32:64, :].bitcast(I32), 0)
         nc.vector.memset(scale_rows[64:P, :].bitcast(I32), 0)
-        load_scale_rows(nc.gpsimd, wv4_plane, 0, wv4_scales[0])
+        load_scale_rows(nc.gpsimd, r8_plane, R8_ROW, r8_scales[0])
         make_identity(nc, ident[:])
 
         nc.sync.dma_start(offsets[:], offs)
@@ -83,38 +81,37 @@ def tile_list_mlat_resid_qf_mask_kernel(
         nc.sync.dma_start(out=x_raw[:], in_=x.rearrange("(p j) m -> p j m", j=PACK))
         load_scale_rows(nc.sync, w4_plane, 0, w4_scales[0])
         nc.sync.dma_start(out=w4[:].bitcast(I32), in_=w4_words[0].bitcast(I32))
-        load_scale_rows(nc.sync, r8_plane, R8_ROW, r8_scales[0], range(1))
         nc.sync.dma_start(out=tab[0][:].bitcast(I32), in_=tab_rows[0])
-        load_scale_rows(nc.sync, r8_plane, R8_ROW, r8_scales[0], range(1, 4))
         nc.sync.dma_start(out=r8[:].bitcast(I32), in_=r8_words[0].rearrange("p r i -> p (r i)").bitcast(I32))
         nc.sync.dma_start(out=wv8_raw[0][:], in_=wv8_rows[:, :, 0 : N // 2])
 
         got_rows = tile("got_rows", [P, J], U8)
         nc.vector.tensor_copy(got_rows[:], scale_rows[:].indirect(offsets[:]))
-        tab_plane = [tile("tab_plane%d" % a, [P, J], U8) for a in range(2)]
-
-        def move_scale_rows(a):
-            for r in range(4):
-                nc.sync.dma_start(
-                    out=tab_plane[a][TAB_ROW[a] + r : P : 32, :].bitcast(I32), in_=got_rows[16 * a + r : 16 * (a + 1) : 4, :].bitcast(I32)
-                )
-
-        move_scale_rows(0)
-        nc.sync.dma_start(out=tab[1][:].bitcast(I32), in_=tab_rows[1])
-        nc.sync.dma_start(out=wv4[:].bitcast(I32), in_=wv4_words[0].bitcast(I32))
-        move_scale_rows(1)
-        nc.sync.dma_start(out=wv8_raw[1][:], in_=wv8_rows[:, :, N // 2 : N])
 
         def quantize(codes, plane, grouped):
             nc.vector.quantize_mx(out=codes.bitcast(E4M3), scales=plane, in_=grouped)
 
-        x_grouped = [tile("x_grouped%d" % t, [P, P, PACK], BF16) for t in range(2)]
+        x_grouped = [tile("x_grouped0", [P, P, PACK], BF16), laid_tile("x_grouped1", [P, P, PACK], BF16, 4 * T - 64)]
         x_codes = [tile("x_codes%d" % t, [P, P], U32) for t in range(2)]
         x_plane = [tile("x_plane%d" % t, [P, P], U8) for t in range(2)]
         for t in range(2):
             interleave(nc.scalar.copy, x_grouped[t][:], x_raw[:, :, t * P : (t + 1) * P])
         for t in range(2):
             quantize(x_codes[t][:], x_plane[t][:], x_grouped[t][:].rearrange("p m j -> p (m j)"))
+
+        planes = [tile("planes0", [P, J], U8), tile("planes1", [P, J + N], U8)]
+        tab_plane = [planes[a][:, 0:J] for a in range(2)]
+        wv4_plane = planes[1][:, J : J + N]
+        staged = laid_tile("staged", [P, J + N], U8, 4 * T)
+
+        def move_scale_rows(a, rows):
+            for r in range(4):
+                nc.sync.dma_start(out=planes[a][TAB_ROW[a] + r : P : 32, :].bitcast(I32), in_=rows[16 * a + r : 16 * (a + 1) : 4, :].bitcast(I32))
+
+        move_scale_rows(0, got_rows)
+        nc.sync.dma_start(out=staged[16:32, J : J + N].bitcast(I32), in_=wv4_scales[0].bitcast(I32))
+        nc.vector.tensor_copy(staged[0:32, 0:J].bitcast(I32), got_rows[0:32, :].bitcast(I32))
+        nc.sync.dma_start(out=tab[1][:].bitcast(I32), in_=tab_rows[1])
 
         lists = [offsets[:, h * (HALF // 16) : (h + 1) * (HALF // 16)] for h in range(2)]
         halves = [slice(h * HALF, (h + 1) * HALF) for h in range(2)]
@@ -137,9 +134,11 @@ def tile_list_mlat_resid_qf_mask_kernel(
                     rhs=r8[:, BANK * a : BANK * (a + 1)].bitcast(E4M3), rhs_scale=r8_plane[R8_ROW:, BANK * a : BANK * (a + 1)],
                     start=False, stop=True,
                 )
-        mask = [tile("mask%d" % t, [P, J], F32, ("w4", "r8")[t]) for t in range(2)]
-        for t in range(2):
-            nc.sync.dma_start(out=mask[t][:], in_=msk[t * P : (t + 1) * P, :])
+        wv4 = tile("wv4", [P, 2 * N], U8, "w4")
+        nc.sync.dma_start(out=wv4[:].bitcast(I32), in_=wv4_words[0].bitcast(I32))
+        move_scale_rows(1, staged)
+        wv8_raw.append(tile("wv8_raw1", [P, PACK, N // 2], F32, "r8"))
+        nc.sync.dma_start(out=wv8_raw[1][:], in_=wv8_rows[:, :, N // 2 : N])
 
         def empty_qa(t, a, copy):
             qa_rows[t, a] = tile("qa_rows%d%d" % (t, a), [P, 2, P, 2], BF16)
@@ -156,7 +155,7 @@ def tile_list_mlat_resid_qf_mask_kernel(
 
         turned = {}
         qa_grouped = {}
-        qa_codes = [laid_tile("qa_codes0", [P, 2 * P], U32, 2048), tile("qa_codes1", [P, 2 * P], U32, "w4")]
+        qa_codes = [laid_tile("qa_codes0", [P, 2 * P], U32, 2048), tile("qa_codes1", [P, 2 * P], U32, "wv8_raw0")]
         qa_plane = [tile("qa_plane%d" % t, [P, 2 * P], U8) for t in range(2)]
 
         def turn_qa(t):
@@ -235,6 +234,9 @@ def tile_list_mlat_resid_qf_mask_kernel(
         gather_half(0, 1)
         interleave(nc.vector.tensor_copy, wv8_grouped[0][:], wv8_raw[0][:])
         quantize_wv8(0)
+        mask = [tile("mask%d" % t, [P, J], F32, ("wv8_raw0", "wv8_grouped0")[t]) for t in range(2)]
+        for t in range(2):
+            nc.sync.dma_start(out=mask[t][:], in_=msk[t * P : (t + 1) * P, :])
         for t in range(2):
             for a in range(2):
                 empty_qa(t, a, nc.scalar.copy)

@@ -73,7 +73,6 @@ def tile_list_mlat_resid_qf_mask_kernel(
 
         nc.vector.memset(scale_rows[32:64, :].bitcast(I32), 0)
         nc.vector.memset(scale_rows[64:P, :].bitcast(I32), 0)
-        load_scale_rows(nc.gpsimd, r8_plane, R8_ROW, r8_scales[0])
         make_identity(nc, ident[:])
 
         nc.sync.dma_start(offsets[:], offs)
@@ -81,7 +80,9 @@ def tile_list_mlat_resid_qf_mask_kernel(
         nc.sync.dma_start(out=x_raw[:], in_=x.rearrange("(p j) m -> p j m", j=PACK))
         load_scale_rows(nc.sync, w4_plane, 0, w4_scales[0])
         nc.sync.dma_start(out=w4[:].bitcast(I32), in_=w4_words[0].bitcast(I32))
+        load_scale_rows(nc.sync, r8_plane, R8_ROW, r8_scales[0], range(1))
         nc.sync.dma_start(out=tab[0][:].bitcast(I32), in_=tab_rows[0])
+        load_scale_rows(nc.sync, r8_plane, R8_ROW, r8_scales[0], range(1, 4))
         nc.sync.dma_start(out=r8[:].bitcast(I32), in_=r8_words[0].rearrange("p r i -> p (r i)").bitcast(I32))
         nc.sync.dma_start(out=wv8_raw[0][:], in_=wv8_rows[:, :, 0 : N // 2])
 

from contextlib import ExitStack

import concourse.mybir as mybir
from concourse.masks import make_identity

K, R, M, T, N, J = 512, 1024, 256, 2048, 512, 1024
FLOPS = 2 * (2 * K * R * M + R * M * J + R * N * J)
SCORE_SCALE = 0.03125

F32 = mybir.dt.float32
BF16 = mybir.dt.bfloat16
I32 = mybir.dt.int32
U32 = mybir.dt.uint32
U16 = mybir.dt.uint16
U8 = mybir.dt.uint8
E4M3 = mybir.dt.float8_e4m3fn_x4
E2M1 = mybir.dt.float4_e2m1fn_x4
MULT = mybir.AluOpType.mult
ADD = mybir.AluOpType.add

P = 128
PACK = 4
BANK = 512
HALF = J // 2
TAB_ROW = (4, 0)
R8_ROW = 8


def load_scale_rows(queue, plane, first_row, rows, places=range(4)):
    by_place = rows.rearrange("(q r) n -> r q n", r=4)
    for r in places:
        queue.dma_start(out=plane[first_row + r : P : 32, :].bitcast(I32), in_=by_place[r].bitcast(I32))


def interleave(copy, grouped, raw):
    copy(
        out=grouped.rearrange("p (c i) j -> p c j i", i=4),
        in_=raw.rearrange("p j (c i) -> p c j i", i=4),
    )


def tile_list_mlat_resid_qf_mask_kernel(
    tc, x, w4_words, w4_scales, r8_words, r8_scales, tab_words, tab_scales, wv8, wv4_words, wv4_scales, msk, offs, out_0, out_1
):
    nc = tc.nc
    with ExitStack() as ctx:
        sb = ctx.enter_context(tc.tile_pool(name="sb", bufs=1))
        laid = ctx.enter_context(tc.tile_pool(name="laid", bufs=1))
        ps = ctx.enter_context(tc.psum_pool(name="ps", bufs=1))

        def tile(name, shape, dtype, reuses=None):
            return sb.tile(shape, dtype, name=name, tag=reuses or name, align_bytes=64)

        def laid_tile(name, shape, dtype, offset):
            return laid.tile(shape, dtype, name=name, align_bytes=64, offset=offset)

        def bank(index, shape):
            return ps.tile(shape, F32, name="bank%d" % index, tag="bank%d" % index)

        offsets = sb.tile([P, J // 16], U16, name="offsets")
        w4_plane = tile("w4_plane", [P, R], U8)
        r8_plane = tile("r8_plane", [P, R], U8)
        x_raw = tile("x_raw", [P, PACK, M], F32)
        r8 = tile("r8", [P, R], U32)
        w4 = tile("w4", [P, 2 * R], U8)
        ident = tile("ident", [P, P], F32)
        scale_rows = tile("scale_rows", [P, T], U8)
        tab = [tile("tab0", [P, T], U32), laid_tile("tab1", [P, T], U32, 0)]
        wv8_raw = [tile("wv8_raw0", [P, PACK, N // 2], F32)]

        tab_rows = [tab_words[a].rearrange("p t i -> p (t i)").bitcast(I32) for a in range(2)]
        wv8_rows = wv8.rearrange("(p j) n -> p j n", j=PACK)

        nc.vector.memset(scale_rows[32:64, :].bitcast(I32), 0)
        nc.vector.memset(scale_rows[64:P, :].bitcast(I32), 0)
        make_identity(nc, ident[:])

        nc.sync.dma_start(offsets[:], offs)
        nc.sync.dma_start(out=scale_rows[0:32, :].bitcast(I32), in_=tab_scales.rearrange("a b t -> (a b) t").bitcast(I32))
        nc.sync.dma_start(out=x_raw[:], in_=x.rearrange("(p j) m -> p j m", j=PACK))
        load_scale_rows(nc.sync, w4_plane, 0, w4_scales[0])
        nc.sync.dma_start(out=w4[:].bitcast(I32), in_=w4_words[0].bitcast(I32))
        load_scale_rows(nc.sync, r8_plane, R8_ROW, r8_scales[0], range(1))
        nc.sync.dma_start(out=tab[0][:].bitcast(I32), in_=tab_rows[0])
        load_scale_rows(nc.sync, r8_plane, R8_ROW, r8_scales[0], range(1, 4))
        nc.sync.dma_start(out=r8[:].bitcast(I32), in_=r8_words[0].rearrange("p r i -> p (r i)").bitcast(I32))
        nc.sync.dma_start(out=wv8_raw[0][:], in_=wv8_rows[:, :, 0 : N // 2])

        got_rows = tile("got_rows", [P, J], U8)
        nc.vector.tensor_copy(got_rows[:], scale_rows[:].indirect(offsets[:]))

        def quantize(codes, plane, grouped):
            nc.vector.quantize_mx(out=codes.bitcast(E4M3), scales=plane, in_=grouped)

        x_grouped = [tile("x_grouped0", [P, P, PACK], BF16), laid_tile("x_grouped1", [P, P, PACK], BF16, 4 * T - 64)]
        x_codes = [tile("x_codes%d" % t, [P, P], U32) for t in range(2)]
        x_plane = [tile("x_plane%d" % t, [P, P], U8) for t in range(2)]
        for t in range(2):
            interleave(nc.scalar.copy, x_grouped[t][:], x_raw[:, :, t * P : (t + 1) * P])
        for t in range(2):
            quantize(x_codes[t][:], x_plane[t][:], x_grouped[t][:].rearrange("p m j -> p (m j)"))

        planes = [tile("planes0", [P, J], U8), tile("planes1", [P, J + N], U8)]
        tab_plane = [planes[a][:, 0:J] for a in range(2)]
        wv4_plane = planes[1][:, J : J + N]
        staged = laid_tile("staged", [P, J + N], U8, 4 * T)

        def move_scale_rows(a, rows):
            for r in range(4):
                nc.sync.dma_start(out=planes[a][TAB_ROW[a] + r : P : 32, :].bitcast(I32), in_=rows[16 * a + r : 16 * (a + 1) : 4, :].bitcast(I32))

        move_scale_rows(0, got_rows)
        nc.sync.dma_start(out=staged[16:32, J : J + N].bitcast(I32), in_=wv4_scales[0].bitcast(I32))
        nc.vector.tensor_copy(staged[0:32, 0:J].bitcast(I32), got_rows[0:32, :].bitcast(I32))
        nc.sync.dma_start(out=tab[1][:].bitcast(I32), in_=tab_rows[1])

        lists = [offsets[:, h * (HALF // 16) : (h + 1) * (HALF // 16)] for h in range(2)]
        halves = [slice(h * HALF, (h + 1) * HALF) for h in range(2)]
        got = {}

        qa_acc = {}
        for t in range(2):
            for a in range(2):
                qa_acc[t, a] = bank(2 * t + a, [P, BANK])
                nc.tensor.matmul_mx(
                    out=qa_acc[t, a][:], lhsT=x_codes[t][:].bitcast(E4M3), lhsT_scale=x_plane[t][:],
                    rhs=w4[:, 2 * BANK * a : 2 * BANK * (a + 1)].bitcast(E2M1), rhs_scale=w4_plane[:, BANK * a : BANK * (a + 1)],
                    start=True, stop=False,
                )
        qa_rows = {}
        for t in range(2):
            for a in range(2):
                nc.tensor.matmul_mx(
                    out=qa_acc[t, a][:], lhsT=x_codes[t][:].bitcast(E4M3), lhsT_scale=x_plane[t][:],
                    rhs=r8[:, BANK * a : BANK * (a + 1)].bitcast(E4M3), rhs_scale=r8_plane[R8_ROW:, BANK * a : BANK * (a + 1)],
                    start=False, stop=True,
                )
        wv4 = tile("wv4", [P, 2 * N], U8, "w4")
        nc.sync.dma_start(out=wv4[:].bitcast(I32), in_=wv4_words[0].bitcast(I32))
        move_scale_rows(1, staged)
        wv8_raw.append(tile("wv8_raw1", [P, PACK, N // 2], F32, "r8"))
        nc.sync.dma_start(out=wv8_raw[1][:], in_=wv8_rows[:, :, N // 2 : N])

        def empty_qa(t, a, copy):
            qa_rows[t, a] = tile("qa_rows%d%d" % (t, a), [P, 2, P, 2], BF16)
            copy(out=qa_rows[t, a][:], in_=qa_acc[t, a][:].rearrange("m (p u e) -> m u p e", u=2, e=2))

        wv8_grouped = [tile("wv8_grouped0", [P, 2 * P, PACK], BF16), laid_tile("wv8_grouped1", [P, 2 * P, PACK], BF16, 0)]
        half_codes = [tile("wv8_codes%d" % g, [P, 2 * P], U32) for g in range(2)]
        half_plane = [tile("wv8_plane%d" % g, [P, 2 * P], U8) for g in range(2)]
        wv8_codes = [half_codes[n // 2][:, (n % 2) * P : (n % 2 + 1) * P] for n in range(4)]
        wv8_plane = [half_plane[n // 2][:, (n % 2) * P : (n % 2 + 1) * P] for n in range(4)]

        def quantize_wv8(g):
            quantize(half_codes[g][:], half_plane[g][:], wv8_grouped[g][:].rearrange("p n j -> p (n j)"))

        turned = {}
        qa_grouped = {}
        qa_codes = [laid_tile("qa_codes0", [P, 2 * P], U32, 2048), tile("qa_codes1", [P, 2 * P], U32, "wv8_raw0")]
        qa_plane = [tile("qa_plane%d" % t, [P, 2 * P], U8) for t in range(2)]

        def turn_qa(t):
            turned[t] = bank(4 * t, [P, 2, 2, P])
            for a in range(2):
                pairs = qa_rows[t, a][:].rearrange("m u p e -> m (u p e)").bitcast(F32)
                for u in range(2):
                    nc.tensor.transpose(turned[t][:, a, u, :], pairs[:, u * P : (u + 1) * P], ident[:])
            qa_grouped[t] = tile("qa_grouped%d" % t, [P, 2 * P * PACK], BF16)
            nc.scalar.copy(
                out=qa_grouped[t][:].bitcast(F32).rearrange("p (a m u) -> p a m u", a=2, u=2),
                in_=turned[t][:].rearrange("p a u m -> p a m u"),
            )

        value_acc = {}
        score_acc = {}
        score_bank = {(0, 0): 1, (0, 1): 2, (1, 0): 7, (1, 1): 4}
        value_bank = {(0, 0): 1, (1, 0): 2, (0, 1): 3, (1, 1): 0, (2, 0): 5, (3, 0): 6, (2, 1): 3, (3, 1): 0}

        def wv4_pass(n, h, opens):
            if opens:
                value_acc[n, h] = bank(value_bank[n, h], [P, BANK])
            nc.tensor.matmul_mx(
                out=value_acc[n, h][:], lhsT=wv4[:, 2 * P * n : 2 * P * (n + 1)].bitcast(E2M1),
                lhsT_scale=wv4_plane[:, P * n : P * (n + 1)],
                rhs=got[1, h].bitcast(E4M3), rhs_scale=tab_plane[1][:, halves[h]], start=opens, stop=not opens,
            )

        def wv8_pass(n, h, opens):
            if opens:
                value_acc[n, h] = bank(value_bank[n, h], [P, BANK])
            nc.tensor.matmul_mx(
                out=value_acc[n, h][:], lhsT=wv8_codes[n].bitcast(E4M3), lhsT_scale=wv8_plane[n],
                rhs=got[0, h].bitcast(E4M3), rhs_scale=tab_plane[0][TAB_ROW[0] :, halves[h]], start=opens, stop=not opens,
            )

        def store_values(n, h, copy):
            result = tile("values%d%d" % (n, h), [P, HALF], F32)
            copy(out=result[:], in_=value_acc[n, h][:])
            nc.sync.dma_start(out=out_1[n * P : (n + 1) * P, halves[h]], in_=result[:])

        def store_value_rows(n, copies):
            result = tile("values%d" % n, [P, J], F32)
            for h in range(2):
                wv8_pass(n, h, False)
                copies[h](out=result[:, halves[h]], in_=value_acc[n, h][:])
            nc.sync.dma_start(out=out_1[n * P : (n + 1) * P, :], in_=result[:])

        def score_pass(t, h, a):
            if a == 0:
                score_acc[t, h] = bank(score_bank[t, h], [P, BANK])
            nc.tensor.matmul_mx(
                out=score_acc[t, h][:], lhsT=qa_codes[t][:, P * a : P * (a + 1)].bitcast(E4M3),
                lhsT_scale=qa_plane[t][:, P * a : P * (a + 1)],
                rhs=got[a, h].bitcast(E4M3), rhs_scale=tab_plane[a][TAB_ROW[a] :, halves[h]], start=(a == 0), stop=(a == 1),
            )

        def store_scores(t, whole):
            result = tile("scores%d" % t, [P, J], F32)
            for h in range(2):
                score_pass(t, h, 0)
                score_pass(t, h, 1)
                nc.vector.scalar_tensor_tensor(
                    out=result[:, halves[h]], in0=score_acc[t, h][:], scalar=SCORE_SCALE, in1=mask[t][:, halves[h]], op0=MULT, op1=ADD
                )
                if not whole:
                    nc.sync.dma_start(out=out_0[t * P : (t + 1) * P, halves[h]], in_=result[:, halves[h]])
            if whole:
                nc.sync.dma_start(out=out_0[t * P : (t + 1) * P, :], in_=result[:])

        def gather_half(a, h):
            got[a, h] = tile("got%d%d" % (a, h), [P, HALF], U32)[:]
            nc.vector.tensor_copy(got[a, h], tab[a][:].indirect(lists[h]))

        gather_half(0, 0)
        gather_half(0, 1)
        interleave(nc.vector.tensor_copy, wv8_grouped[0][:], wv8_raw[0][:])
        quantize_wv8(0)
        mask = [tile("mask%d" % t, [P, J], F32, ("wv8_raw0", "wv8_grouped0")[t]) for t in range(2)]
        for t in range(2):
            nc.sync.dma_start(out=mask[t][:], in_=msk[t * P : (t + 1) * P, :])
        for t in range(2):
            for a in range(2):
                empty_qa(t, a, nc.scalar.copy)
        turn_qa(0)
        for n in range(2):
            wv8_pass(n, 0, True)
        turn_qa(1)
        for n in range(2):
            wv8_pass(n, 1, True)
        gather_half(1, 0)
        gather_half(1, 1)
        quantize(qa_codes[0][:], qa_plane[0][:], qa_grouped[0][:])
        interleave(nc.vector.tensor_copy, wv8_grouped[1][:], wv8_raw[1][:])
        for h in range(2):
            for n in range(2):
                wv4_pass(n, h, False)
                store_values(n, h, nc.scalar.copy)
            if h == 0:
                for n in range(2, 4):
                    wv4_pass(n, 0, True)
        quantize_wv8(1)
        store_scores(0, False)
        quantize(qa_codes[1][:], qa_plane[1][:], qa_grouped[1][:])
        for n in range(2, 4):
            wv4_pass(n, 1, True)
            store_value_rows(n, (nc.scalar.copy, nc.scalar.copy))
        store_scores(1, True)
